import numpy as np, ml_dtypes
CORES = [78,86,94,102,110,118]
N = 6
import mx_ref
BF = ml_dtypes.bfloat16
def entries(a):
    return np.ascontiguousarray(a.T).reshape(-1)
def table(e):
    return np.ascontiguousarray(np.reshape(e, (-1, 16)).T).astype(np.int32)
def f(rng, *shape):
    return mx_ref.flush((rng.standard_normal(shape, dtype=np.float32) * np.exp2(rng.integers(-2, 3, shape[:-1] + (1,)))).astype(BF))
def wide(rng, *shape, cols=0):
    v = rng.standard_normal(shape, dtype=np.float32) * np.exp2(rng.integers(-12, 13, shape)).astype(np.float32)
    if cols: v *= np.repeat(np.exp2(rng.integers(-cols, cols + 1, shape[:-2] + (1, shape[-1] // 4))) * (rng.random(shape[:-2] + (1, shape[-1] // 4)) > 0.0625), 4, axis=-1).astype(np.float32)
    return mx_ref.flush(v.astype(BF))
SH, CH, RD = 128, 64, 4
def lists(rng, same=False, apart=False, ends=False):
    a = []
    for r in range(N):
        p = rng.permutation(SH); e = []
        for t in range(1, RD):
            if same: c = p[:CH]
            elif apart: c = p[np.arange(CH * (t - 1), CH * t) % SH]
            elif ends: c = np.concatenate([[0, SH - 1], 1 + rng.permutation(SH - 2)[:CH - 2]])
            else: c = rng.permutation(SH)[:CH]
            e.append(rng.permutation(c))
        a.append(table(np.concatenate(e)))
    return {"idx": np.stack(a)}
def setup_inputs(rng):
    return {"wm": f(rng, N, 128, 4 * SH), "dl": f(rng, N, 128, (RD - 1) * 4 * CH), **lists(rng), "x": f(rng, N, 128, RD * 512)}
def setup_inputs_same(rng):
    return {**setup_inputs(rng), **lists(rng, same=True)}
def setup_inputs_apart(rng):
    return {**setup_inputs(rng), **lists(rng, apart=True)}
def setup_inputs_ends(rng):
    return {**setup_inputs(rng), **lists(rng, ends=True)}
def setup_inputs_big(rng):
    d = setup_inputs(rng); d["dl"] = (d["dl"].astype(np.float32) * np.float32(256)).astype(BF); return d
def setup_inputs_spread(rng):
    d = setup_inputs(rng); d["wm"] = wide(rng, N, 128, 4 * SH, cols=8); d["dl"] = wide(rng, N, 128, (RD - 1) * 4 * CH, cols=8); return d
def check_inputs(d):
    b = []
    for r in range(N):
        e = entries(d["idx"][r])
        if e.min() < 0 or e.max() >= SH: b.append("idx: range")
        for t in range(1, RD):
            if len(set(e[CH * (t - 1):CH * t].tolist())) != CH: b.append("idx: a column twice in one round")
    return b
def reference(wm, dl, idx, x):
    W = []
    for q in range(N):
        m = wm[q].reshape(128, SH, 4).copy(); d = dl[q].reshape(128, (RD - 1) * CH, 4); e = entries(idx[q])
        W.append([mx_ref.quantize(wm[q])])
        for t in range(1, RD):
            s = slice(CH * (t - 1), CH * t)
            m[:, e[s]] = (m[:, e[s]].astype(np.float32) + np.float32(0.25) * d[:, s].astype(np.float32)).astype(BF)
            W[q].append(mx_ref.quantize(m.reshape(128, 4 * SH).copy()))
    y = np.zeros((N, 128, RD * N * SH), np.float32)
    for r in range(N):
        for t in range(RD):
            X = mx_ref.quantize(np.ascontiguousarray(x[r][:, 512 * t:512 * t + 512]))
            for q in range(N):
                k = t * N + q
                y[r][:, SH * k:SH * k + SH] = mx_ref.matmul(X, W[q][t])
    return {"y": y}

@@ -1,0 +1,436 @@
+import numpy as np
+from concourse.bass import DstId, RemoteDMATransfer
+from concourse.mybir import dt, AluOpType, ActivationFunctionType
+
+N, SH, CH, RD = 6, 128, 64, 4
+NP = N // 2
+WIN = 2 * SH + 2 * 3 * CH
+F8 = "float8_e4m3fn_x4"
+
+SCRATCH = {
+    "md": ("sbuf", [128, 4 * WIN], "bfloat16"),
+    "dlt": ("sbuf", [128, 3 * 4 * CH], "bfloat16"),
+    "dls": ("sbuf", [128, 3 * 4 * CH], "bfloat16"),
+    "xt": ("sbuf", [128, RD * 512], "bfloat16"),
+    "xq": ("sbuf", [128, RD * 128], F8),
+    "xs": ("sbuf", [128, RD * 128], "uint8"),
+    "wl": ("sbuf", [128, N * SH], F8),
+    "ws": ("sbuf", [128, N * SH], "uint8"),
+    "dq": ("sbuf", [128, N * 3 * CH], F8),
+    "dp": ("sbuf", [128, N * 3 * CH], "uint8"),
+    "hw": ("sbuf", [128, SH], F8),
+    "hws": ("sbuf", [128, SH], "uint8"),
+    "hd": ("sbuf", [128, 3 * CH], F8),
+    "hds": ("sbuf", [128, 3 * CH], "uint8"),
+    "ix": ("sbuf", [128, 12], "int32"),
+    "lo": ("sbuf", [128, 12], "int32"),
+    "hi": ("sbuf", [128, 12], "int32"),
+    "lm": ("sbuf", [128, 12], "int32"),
+    "sm": ("sbuf", [128, 12], "int32"),
+    "piu": ("sbuf", [128, 12], "uint16"),
+    "o1": ("sbuf", [128, 16], "uint16"),
+    "o2": ("sbuf", [128, 16], "uint16"),
+    "o3": ("sbuf", [128, 16], "uint16"),
+    "mi": ("sbuf", [128, CH], "int32"),
+    "mj": ("sbuf", [128, CH], "int32"),
+    "mk": ("sbuf", [128, CH], "float32"),
+    "rm": ("sbuf", [128, CH], "float32"),
+    "pi": ("sbuf", [128, 1], "int32"),
+    "pe": ("sbuf", [128, 1], "int32"),
+    "e1": ("sbuf", [128, 1], "float32"),
+    "e2": ("sbuf", [128, 1], "float32"),
+    "e3": ("sbuf", [128, 1], "float32"),
+    "vl": ("sbuf", [128, 3 * CH], "float32"),
+    "lw": ("sbuf", [128, 3 * SH], "float32"),
+    "k1": ("sbuf", [128, CH], "float32"),
+    "k2": ("sbuf", [128, CH], "float32"),
+    "k3": ("sbuf", [128, CH], "float32"),
+    "c1": ("sbuf", [128, CH], "float32"),
+    "c2": ("sbuf", [128, CH], "float32"),
+    "c3": ("sbuf", [128, CH], "float32"),
+    "lu": ("sbuf", [128, 3 * SH], "uint16"),
+    "lsend": ("dram", [128, 3], "uint16"),
+    "lland": ("dram", [N * 128, 3], "uint16"),
+    "comb": ("dram", [16, 3, 8 * N], "uint16"),
+    "offs": ("sbuf", [128, 3 * 8 * N], "uint16"),
+    "pw1": ("sbuf", [128, NP * WIN], "float32"),
+    "pw2": ("sbuf", [128, NP * WIN], "float32"),
+    "pw3": ("sbuf", [128, NP * WIN], "float32"),
+    "y0": ("sbuf", [128, N * SH], "float32"),
+    "y1": ("sbuf", [128, N * SH], "float32"),
+    "y2": ("sbuf", [128, N * SH], "float32"),
+    "y3": ("sbuf", [128, N * SH], "float32"),
+    "pb": ("psum", [128, 512 * 8], "float32"),
+}
+SEMAPHORES = (["vs", "ss", "ps", "gs", "lix", "lwm", "ldl", "lx", "lbo", "st1", "st2", "sty", "stz", "loc", "lst",
+               "hwc", "hwp", "hdc", "hdp"]
+              + ["w%d" % q for q in range(N)] + ["d%d" % q for q in range(N)])
+
+
+def bits(engines):
+    m = 0
+    for e in engines:
+        m |= 1 << e
+    return m
+
+
+def links(src, dst, topo):
+    a, b, d = topo.chip(src), topo.chip(dst), topo.die(src)
+    out = []
+    if not topo.same_plane(a, b):
+        m = [c for c in range(topo.CHIPS) if topo.mates(a, c)][0]
+        out.append(("mate", d, a))
+        a = m
+    if a != b:
+        out.append(("out", d, a))
+        out.append(("in", d, b))
+    return out
+
+
+def helpers(core, dsts, topo):
+    ok = [c for c in topo.cores_of(core) if c != core and all(topo.may_write(c, d) for d in dsts)]
+    near = [c for c in ok if topo.die(c) == topo.die(core)]
+    far = [c for c in ok if topo.die(c) != topo.die(core)]
+    return near[0], far[0]
+
+
+def routes(cores, topo):
+    hp = [helpers(c, [d for d in cores if d != c], topo) for c in cores]
+    far = [[(q + 2) % N, (q + 4) % N] for q in range(N)]
+
+    def cost(sel):
+        load = {}
+        for q in range(N):
+            for r in range(N):
+                if r != q:
+                    s = hp[q][1] if r in sel[q] else cores[q]
+                    for k in links(s, cores[r], topo):
+                        load[k] = load.get(k, 0) + 1
+        return (max(load.values()), sum(v * v for v in load.values()))
+
+    best = cost(far)
+    moved = True
+    while moved:
+        moved = False
+        for q in range(N):
+            for a in range(N):
+                for b in range(a + 1, N):
+                    if q in (a, b):
+                        continue
+                    for q2 in range(N):
+                        for a2 in range(N):
+                            for b2 in range(a2 + 1, N):
+                                if q2 in (a2, b2) or (q2 == q and (a2, b2) != (a, b)) or q2 < q:
+                                    continue
+                                t = [list(f) for f in far]
+                                t[q], t[q2] = [a, b], [a2, b2]
+                                c = cost(t)
+                                if c < best:
+                                    best, far, moved = c, t, True
+    near = [[r for r in range(N) if r != q and r not in far[q]] for q in range(N)]
+    pick = None
+    for n in range(3 ** N):
+        ch = [near[q][n // 3 ** q % 3] for q in range(N)]
+        if pick is None or len(set(ch)) > len(set(pick)):
+            pick = ch
+    return [(hp[q][0], hp[q][1], pick[q], [r for r in near[q] if r != pick[q]], far[q]) for q in range(N)]
+
+
+_CACHE = {}
+
+
+def plan(T, topo):
+    if "r" not in _CACHE:
+        _CACHE["r"] = routes(list(T.cores), topo)
+    return _CACHE["r"]
+
+
+def dst_id(c, topo):
+    rid, pid, _ = topo.addr(c)
+    return DstId(rid=rid, pnc=pid)
+
+
+def u8(v):
+    return v.bitcast(dt.uint8)
+
+
+def helper_program(g, core, T, topo, q, ranks):
+    dst = [T.cores[r] for r in ranks]
+    ids = [dst_id(c, topo) for c in dst]
+    eng = [e for e in topo.engines(core, dst[0]) if all(e in topo.engines(core, d) for d in dst)]
+    wc, dc = slice(SH * q, SH * (q + 1)), slice(3 * CH * q, 3 * CH * (q + 1))
+    n = 0
+    for arr, src, out, sem in ((T.sem.hwc, u8(T.hw[:]), u8(T.wl[:, wc]), "w%d" % q),
+                               (T.sem.hwp, T.hws[:], T.ws[:, wc], "w%d" % q),
+                               (T.sem.hdc, u8(T.hd[:]), u8(T.dq[:, dc]), "d%d" % q),
+                               (T.sem.hdp, T.hds[:], T.dp[:, dc], "d%d" % q)):
+        g.wait_ge(arr, 8)
+        g.remote_dma_fused([RemoteDMATransfer(dst_ids=ids, dma_engine_mask=bits(eng), remote_sem=T.sem[sem],
+                                              srcs=[src], dsts=[out for _ in dst])], local_sem=T.sem.loc)
+        n += len(eng)
+    g.wait_ge(T.sem.loc, n)
+
+
+def rank_program(g, core, T, topo):
+    P = plan(T, topo)
+    r = T.rank_of(core)
+    if r is None:
+        for q in range(N):
+            if core == P[q][0]:
+                helper_program(g, core, T, topo, q, P[q][3])
+            if core == P[q][1]:
+                helper_program(g, core, T, topo, q, P[q][4])
+        return
+    near, far, direct, _, _ = P[r]
+    odd = r % 2
+    mcol = 0 if odd else 512
+    dcol = [None] + [(320 + CH * (k - 1)) if odd else (320 - CH * k) for k in (1, 2, 3)]
+    dlow = 320 if odd else 128
+    gap = (128, 320) if odd else (320, 512)
+    org = [None, mcol, 0 if odd else dcol[1], 0 if odd else dcol[2]]
+    end = [None, mcol + SH, dcol[1] + CH if odd else WIN, dcol[2] + CH if odd else WIN]
+    add, mult = AluOpType.add, AluOpType.mult
+    cnt = {"v": 0, "s": 0, "p": 0, "g": 0}
+    sem = {"v": T.sem.vs, "s": T.sem.ss, "p": T.sem.ps, "g": T.sem.gs}
+    queue = {"v": g.vector, "s": g.scalar, "p": g.tensor, "g": g, "y": g.sync}
+    seen = {}
+
+    def done(k, ins):
+        ins.then_inc(sem[k], 1)
+        cnt[k] += 1
+        return cnt[k]
+
+    def wait(on, s, val):
+        key = (on, s)
+        if seen.get(key, 0) < val:
+            seen[key] = val
+            queue[on].wait_ge(sem[s] if s in sem else T.sem[s], val)
+
+    v, sc, y, te = g.vector, g.scalar, g.sync, g.tensor
+    wc, dc = slice(SH * r, SH * (r + 1)), slice(3 * CH * r, 3 * CH * (r + 1))
+
+    for k in range(4):
+        y.dma_start(T.ix[16 * k:16 * k + 16, :], T.idx[:]).then_inc(T.sem.lix, 16)
+        sc.dma_start(T.ix[64 + 16 * k:64 + 16 * k + 16, :], T.idx[:]).then_inc(T.sem.lix, 16)
+    y.dma_start(T.md[:, 4 * mcol:4 * mcol + 512], T.wm[:]).then_inc(T.sem.lwm, 16)
+    sc.dma_start(T.dlt[:], T.dl[:]).then_inc(T.sem.ldl, 16)
+    y.dma_start(T.xt[:], T.x[:]).then_inc(T.sem.lx, 16)
+
+    g_pi = done("g", g.iota(T.pi[:], [[0, 1]], 0, 1))
+    g_mi = done("g", g.iota(T.mi[:], [[-4, CH]], 4 * CH, 1))
+    g_lw = done("g", g.iota(T.lw[:], [[1, 16], [0, 3], [16, 8]], mcol, 0, allow_small_or_imprecise_dtypes=True))
+    g_vl = done("g", g.iota(T.vl[:], [[CH if odd else -CH, 3], [1, CH]], dcol[1], 0, allow_small_or_imprecise_dtypes=True))
+    g_rm = done("g", g.iota(T.rm[:], [[0, 16], [1024, 4]], 0, 0, allow_small_or_imprecise_dtypes=True))
+
+    done("v", v.memset(T.md[:, 4 * gap[0]:4 * gap[1]], 0.0))
+    wait("v", "g", g_mi)
+    v_pe = done("v", v.tensor_scalar(T.pe[:], T.pi[:], 3, None, AluOpType.bitwise_and))
+    v_mj = done("v", v.tensor_scalar(T.mj[:], T.mi[:], 2, 3, AluOpType.arith_shift_right, AluOpType.bitwise_and))
+    wait("v", "v", v_pe)
+    for k in (1, 2, 3):
+        done("v", v.tensor_scalar(T["e%d" % k][:], T.pe[:], -4 * org[k], None, add))
+    wait("v", "v", v_mj)
+    done("v", v.tensor_scalar(T.mk[:], T.mj[:], 0, None, AluOpType.is_equal))
+    wait("v", "lix", 128)
+    v_lo = done("v", v.tensor_scalar(T.lo[:], T.ix[:], 15, None, AluOpType.bitwise_and))
+    done("v", v.tensor_scalar(T.hi[:], T.ix[:], 4, None, AluOpType.arith_shift_right))
+    wait("v", "v", v_lo)
+    a = done("v", v.tensor_scalar(T.lm[:], T.lo[:], 24, None, mult))
+    wait("v", "v", a)
+    a = done("v", v.tensor_tensor(T.sm[:], T.lm[:], T.hi[:], add))
+    wait("v", "v", a)
+    done("v", v.tensor_copy(T.piu[:], T.sm[:]))
+
+    def place(k, t):
+        wait("v", "v", cnt["v"])
+        return done("v", v.tensor_copy(T.lw[:, 8 * (t - 1):3 * SH].indirect(T.piu[:, 4 * (k - 1):4 * k]),
+                                       T.vl[:, CH * (k - 1):CH * k]))
+
+    def look(t, k):
+        wait("v", "v", cnt["v"])
+        return done("v", v.tensor_tensor(T["k%d" % k][:], T.lw[:, 8 * (t - 1):3 * SH].indirect(T.piu[:, 4 * (k - 1):4 * k]),
+                                         T.mk[:], mult))
+
+    wait("v", "g", g_rm)
+    look(3, 1)
+    place(1, 1)
+    look(1, 2)
+    wait("v", "lwm", 16)
+    v_qw = done("v", v.quantize_mx(T.wl[:, wc], T.ws[:, wc], T.md[:, 4 * mcol:4 * mcol + 512]))
+    place(1, 2)
+    place(2, 2)
+    look(2, 3)
+    place(1, 3)
+    place(2, 3)
+    place(3, 3)
+    wait("v", "v", cnt["v"])
+    v_lu = done("v", v.tensor_copy(T.lu[0:1, :], T.lw[0:1, :]))
+    scan = {}
+    for k in (1, 2, 3):
+        scan[k] = done("v", v.tensor_tensor_scan(T["c%d" % k][:], T.rm[:], T["k%d" % k][:], 0.0, AluOpType.min, add))
+    for k in (1, 2, 3):
+        wait("v", "v", scan[k])
+        done("v", v.tensor_scalar(T["o%d" % k][:], T["c%d" % k][:, 3:CH:4], 4, T["e%d" % k][:], mult, add))
+    for k in (1, 2, 3):
+        wait("v", "v", cnt["v"])
+        wait("v", "s", k)
+        done("v", v.tensor_tensor(T.md[:, 4 * dcol[k]:4 * dcol[k] + 4 * CH],
+                                  T.md[:, 4 * org[k]:4 * end[k]].indirect(T["o%d" % k][:]),
+                                  T.dls[:, 4 * CH * (k - 1):4 * CH * k], add))
+    wait("v", "v", cnt["v"])
+    v_qd = done("v", v.quantize_mx(T.dq[:, dc], T.dp[:, dc], T.md[:, 4 * dlow:4 * dlow + 12 * CH]))
+    wait("v", "lx", 16)
+    v_qx = done("v", v.quantize_mx(T.xq[:], T.xs[:], T.xt[:]))
+    for p in range(NP):
+        for t in (1, 2):
+            for lo, hi in ((128, 320 - CH * t), (320 + CH * t, 512)):
+                v_ms = done("v", v.memset(T["pw%d" % t][:, WIN * p + lo:WIN * p + hi], 0.0))
+
+    wait("s", "ldl", 16)
+    for k in range(3):
+        sl = slice(4 * CH * k, 4 * CH * (k + 1))
+        done("s", sc.activation(T.dls[:, sl], T.dlt[:, sl], ActivationFunctionType.Copy, scale=0.25))
+
+    onchip = topo.engines(core, far)
+    ef, en = onchip[0::2], onchip[1::2]
+    drk = T.cores[direct]
+    ed = topo.engines(core, drk)
+    nloc = [0]
+
+    def hand(src, out, s):
+        g.remote_dma_fused([RemoteDMATransfer(dst_ids=[dst_id(far, topo)], dma_engine_mask=bits(ef), remote_sem=T.sem[s],
+                                              srcs=[src], dsts=[out]),
+                            RemoteDMATransfer(dst_ids=[dst_id(near, topo)], dma_engine_mask=bits(en), remote_sem=T.sem[s],
+                                              srcs=[src], dsts=[out])], local_sem=T.sem.loc)
+        nloc[0] += len(ef) + len(en)
+
+    def send(view, s):
+        g.remote_dma_fused([RemoteDMATransfer(dst_ids=[dst_id(drk, topo)], dma_engine_mask=bits(ed), remote_sem=T.sem[s],
+                                              srcs=[view], dsts=[view])], local_sem=T.sem.loc)
+        nloc[0] += len(ed)
+
+    wait("g", "v", v_qw)
+    hand(u8(T.wl[:, wc]), u8(T.hw[:]), "hwc")
+    hand(T.ws[:, wc], T.hws[:], "hwp")
+    send(u8(T.wl[:, wc]), "w%d" % r)
+    send(T.ws[:, wc], "w%d" % r)
+    others = [T.cores[q] for q in range(N) if q != r]
+    land = T.lland[128 * r:128 * (r + 1), :]
+    wait("g", "lbo", 16)
+    g.remote_dma_fused([RemoteDMATransfer(dst_ids=[dst_id(c, topo) for c in others], dma_engine_mask=bits(ed[:1]),
+                                          remote_sem=T.sem.lst, srcs=[T.lsend[:]], dsts=[land for _ in others])],
+                       local_sem=T.sem.loc)
+    nloc[0] += 1
+    wait("g", "v", v_qd)
+    hand(u8(T.dq[:, dc]), u8(T.hd[:]), "hdc")
+    hand(T.dp[:, dc], T.hds[:], "hdp")
+    send(u8(T.dq[:, dc]), "d%d" % r)
+    send(T.dp[:, dc], "d%d" % r)
+
+    wait("y", "v", v_lu)
+    y.dma_start(T.lsend[:], T.lu[0:1, :]).then_inc(T.sem.lbo, 16)
+    wait("y", "lbo", 16)
+    y.dma_start(T.comb[:, :, 8 * r:8 * r + 8], T.lsend[:]).then_inc(T.sem.st1, 16)
+    wait("y", "lst", N - 1)
+    for q in range(N):
+        if q != r:
+            y.dma_start(T.comb[:, :, 8 * q:8 * q + 8], T.lland[128 * q:128 * (q + 1), :]).then_inc(T.sem.st1, 16)
+    wait("y", "st1", 16 * N)
+    for k in range(8):
+        y.dma_start(T.offs[16 * k:16 * k + 16, :], T.comb[:]).then_inc(T.sem.st2, 16)
+
+    order = [(r // 2 + k) % NP for k in range(NP)]
+    units = [("w", p, t) for p in order for t in range(RD)] + [("d", p, t) for p in order for t in (1, 3, 2)]
+    eng = {u: (("s" if u[2] in (0, 2) else "v") if u[0] == "w" else ("v" if u[2] == 3 else "s")) for u in units}
+    bank, use = {}, {"v": 0, "s": 0}
+    for u in units:
+        e = eng[u]
+        bank[u] = (0 if e == "v" else 4) + use[e] % 4
+        use[e] += 1
+    num = {u: i + 1 for i, u in enumerate(units)}
+
+    def ps(u, lo, hi):
+        return T.pb[:, 512 * bank[u] + lo:512 * bank[u] + hi]
+
+    def copy(e, out, in_):
+        return done(e, v.tensor_copy(out, in_) if e == "v" else sc.activation(out, in_, ActivationFunctionType.Copy))
+
+    drained, got, shard = {}, {}, {}
+
+    def drain(e, u):
+        kind, p, t = u
+        wait(e, "p", num[u])
+        if kind == "w" and t == 0:
+            drained[u] = copy(e, T.y0[:, 256 * p:256 * p + 256], ps(u, 0, 256))
+        elif kind == "w":
+            copy(e, T["pw%d" % t][:, WIN * p + 512:WIN * p + 640], ps(u, 0, 128))
+            drained[u] = copy(e, T["pw%d" % t][:, WIN * p:WIN * p + 128], ps(u, 128, 256))
+            shard[(p, t)] = (e, drained[u])
+        else:
+            drained[u] = copy(e, T["pw%d" % t][:, WIN * p + 320 - CH * t:WIN * p + 320 + CH * t], ps(u, 0, 128 * t))
+
+    def gather(e, p, t):
+        wait(e, "st2", 128)
+        wait(e, "v", v_ms)
+        wait(e, shard[(p, t)][0], shard[(p, t)][1])
+        wait(e, eng[("d", p, t)], drained[("d", p, t)])
+        win = T["pw%d" % t][:, WIN * p:WIN * p + WIN].indirect(T.offs[:, 48 * (t - 1) + 16 * p:48 * (t - 1) + 16 * p + 16])
+        got[(p, t)] = (e, copy(e, T["y%d" % t][:, 256 * p:256 * p + 256], win))
+
+    for p in order:
+        drain("s", ("w", p, 0))
+        drain("s", ("w", p, 2))
+        wait("s", "s", drained[("w", p, 0)])
+        sc.dma_start(T.y[:, 256 * p:256 * p + 256], T.y0[:, 256 * p:256 * p + 256]).then_inc(T.sem.sty, 16)
+        drain("v", ("w", p, 1))
+        drain("v", ("w", p, 3))
+    A, B, C = order
+    for p in (A, B):
+        drain("s", ("d", p, 1))
+        drain("s", ("d", p, 2))
+        drain("v", ("d", p, 3))
+    gather("v", A, 1)
+    gather("v", A, 3)
+    gather("s", A, 2)
+    gather("v", B, 3)
+    gather("s", B, 1)
+    gather("s", B, 2)
+    drain("s", ("d", C, 1))
+    drain("s", ("d", C, 2))
+    drain("v", ("d", C, 3))
+    gather("s", C, 2)
+    gather("v", C, 1)
+    gather("v", C, 3)
+
+    wait("p", "v", v_qx)
+    last = {}
+    for u in units:
+        kind, p, t = u
+        for q in (2 * p, 2 * p + 1):
+            if q != r:
+                wait("p", ("w%d" if kind == "w" else "d%d") % q, 16)
+        b = bank[u]
+        if b in last:
+            wait("p", eng[u], drained[last[b]])
+        last[b] = u
+        if kind == "w":
+            n, lo = 256, 256 * p
+            codes, scales = T.wl, T.ws
+        else:
+            n, lo = 128 * t, 384 * p + 192 - CH * t
+            codes, scales = T.dq, T.dp
+        done("p", te.matmul_mx(ps(u, 0, n), T.xq[:, 128 * t:128 * t + 128], T.xs[:, 128 * t:128 * t + 128],
+                               codes[:, lo:lo + n], scales[:, lo:lo + n], True, True))
+
+    for p, t in ((A, 1), (A, 2), (A, 3), (B, 1), (B, 3), (B, 2), (C, 1), (C, 2), (C, 3)):
+        e, k = got[(p, t)]
+        wait("y", e, k)
+        y.dma_start(T.y[:, SH * N * t + 256 * p:SH * N * t + 256 * p + 256],
+                    T["y%d" % t][:, 256 * p:256 * p + 256]).then_inc(T.sem.stz, 16)
+
+    wait("g", "loc", nloc[0])
+    for k in ("g", "v", "s", "p"):
+        wait("g", k, cnt[k])
+    wait("g", "st2", 128)
+    wait("g", "sty", 16 * NP)
+    wait("g", "stz", 16 * 3 * NP)

@@ -4,67 +4,65 @@ from concourse.mybir import dt, AluOpType, ActivationFunctionType
 
 N, SH, CH, RD = 6, 128, 64, 4
 NP = N // 2
-WIN = 2 * SH + 2 * 3 * CH
+S1, S2 = 2 * SH + 4 * CH, 4 * CH
+BIG = 1024.0
 F8 = "float8_e4m3fn_x4"
+PIECES = "ABCDE"
+
+
+def win(t):
+    return 2 * SH + 2 * CH * t
+
 
 SCRATCH = {
-    "md": ("sbuf", [128, 4 * WIN], "bfloat16"),
+    "md": ("sbuf", [128, 4 * (SH + 3 * CH)], "bfloat16"),
     "dlt": ("sbuf", [128, 3 * 4 * CH], "bfloat16"),
     "dls": ("sbuf", [128, 3 * 4 * CH], "bfloat16"),
     "xt": ("sbuf", [128, RD * 512], "bfloat16"),
     "xq": ("sbuf", [128, RD * 128], F8),
     "xs": ("sbuf", [128, RD * 128], "uint8"),
-    "wl": ("sbuf", [128, N * SH], F8),
-    "ws": ("sbuf", [128, N * SH], "uint8"),
-    "dq": ("sbuf", [128, N * 3 * CH], F8),
-    "dp": ("sbuf", [128, N * 3 * CH], "uint8"),
-    "hw": ("sbuf", [128, SH], F8),
-    "hws": ("sbuf", [128, SH], "uint8"),
-    "hd": ("sbuf", [128, 3 * CH], F8),
-    "hds": ("sbuf", [128, 3 * CH], "uint8"),
+    "c1": ("sbuf", [128, NP * S1], F8),
+    "p1": ("sbuf", [128, NP * S1], "uint8"),
+    "c2": ("sbuf", [128, NP * S2], F8),
+    "p2": ("sbuf", [128, NP * S2], "uint8"),
     "ix": ("sbuf", [128, 12], "int32"),
-    "lo": ("sbuf", [128, 12], "int32"),
-    "hi": ("sbuf", [128, 12], "int32"),
-    "lm": ("sbuf", [128, 12], "int32"),
-    "sm": ("sbuf", [128, 12], "int32"),
-    "piu": ("sbuf", [128, 12], "uint16"),
-    "o1": ("sbuf", [128, 16], "uint16"),
+    "o1": ("sbuf", [128, 12], "uint16"),
+    "o4": ("sbuf", [128, 4], "uint16"),
     "o2": ("sbuf", [128, 16], "uint16"),
     "o3": ("sbuf", [128, 16], "uint16"),
-    "mi": ("sbuf", [128, CH], "int32"),
-    "mj": ("sbuf", [128, CH], "int32"),
-    "mk": ("sbuf", [128, CH], "float32"),
-    "rm": ("sbuf", [128, CH], "float32"),
     "pi": ("sbuf", [128, 1], "int32"),
+    "pa": ("sbuf", [128, 1], "int32"),
     "pe": ("sbuf", [128, 1], "int32"),
-    "e1": ("sbuf", [128, 1], "float32"),
+    "pf": ("sbuf", [128, 1], "float32"),
+    "lc": ("sbuf", [128, 1], "float32"),
+    "ec": ("sbuf", [128, 1], "float32"),
     "e2": ("sbuf", [128, 1], "float32"),
     "e3": ("sbuf", [128, 1], "float32"),
+    "jj": ("sbuf", [128, 3], "int32"),
+    "co": ("sbuf", [128, 4], "uint16"),
+    "mi": ("sbuf", [128, 176], "int32"),
+    "mj": ("sbuf", [128, 176], "int32"),
+    "ma": ("sbuf", [128, 176], "float32"),
+    "mb": ("sbuf", [128, 176], "float32"),
+    "cs": ("sbuf", [128, 176], "float32"),
     "vl": ("sbuf", [128, 3 * CH], "float32"),
-    "lw": ("sbuf", [128, 3 * SH], "float32"),
-    "k1": ("sbuf", [128, CH], "float32"),
-    "k2": ("sbuf", [128, CH], "float32"),
-    "k3": ("sbuf", [128, CH], "float32"),
-    "c1": ("sbuf", [128, CH], "float32"),
-    "c2": ("sbuf", [128, CH], "float32"),
-    "c3": ("sbuf", [128, CH], "float32"),
-    "lu": ("sbuf", [128, 3 * SH], "uint16"),
-    "lsend": ("dram", [128, 3], "uint16"),
+    "tb": ("sbuf", [128, 3 * SH], "float32"),
+    "lk": ("sbuf", [128, 176], "float32"),
+    "sn": ("sbuf", [128, 176], "float32"),
+    "ls": ("sbuf", [128, 3], "uint16"),
     "lland": ("dram", [N * 128, 3], "uint16"),
-    "comb": ("dram", [16, 3, 8 * N], "uint16"),
-    "offs": ("sbuf", [128, 3 * 8 * N], "uint16"),
-    "pw1": ("sbuf", [128, NP * WIN], "float32"),
-    "pw2": ("sbuf", [128, NP * WIN], "float32"),
-    "pw3": ("sbuf", [128, NP * WIN], "float32"),
+    "offs": ("sbuf", [128, 3, 8 * N], "uint16"),
+    "pw1": ("sbuf", [128, NP * win(1)], "float32"),
+    "pw2": ("sbuf", [128, NP * win(2)], "float32"),
+    "pw3": ("sbuf", [128, NP * win(3)], "float32"),
     "y0": ("sbuf", [128, N * SH], "float32"),
     "y1": ("sbuf", [128, N * SH], "float32"),
     "y2": ("sbuf", [128, N * SH], "float32"),
     "y3": ("sbuf", [128, N * SH], "float32"),
     "pb": ("psum", [128, 512 * 8], "float32"),
 }
-SEMAPHORES = (["vs", "ss", "ps", "gs", "lix", "lwm", "ldl", "lx", "lbo", "st1", "st2", "sty", "stz", "loc", "lst",
-               "hwc", "hwp", "hdc", "hdp"]
-              + ["w%d" % q for q in range(N)] + ["d%d" % q for q in range(N)])
+SEMAPHORES = (["vs", "ss", "ps", "gs", "lix", "lwm", "ld1", "ld2", "lx", "lbo", "st2", "stz", "loc", "lst"]
+              + ["a%s%d" % (p, q) for p in PIECES for q in range(N)])
 
 
 def bits(engines):
@@ -74,66 +72,32 @@ def bits(engines):
     return m
 
 
-def links(src, dst, topo):
-    a, b, d = topo.chip(src), topo.chip(dst), topo.die(src)
-    out = []
-    if not topo.same_plane(a, b):
-        m = [c for c in range(topo.CHIPS) if topo.mates(a, c)][0]
-        out.append(("mate", d, a))
-        a = m
-    if a != b:
-        out.append(("out", d, a))
-        out.append(("in", d, b))
-    return out
-
-
-def helpers(core, dsts, topo):
-    ok = [c for c in topo.cores_of(core) if c != core and all(topo.may_write(c, d) for d in dsts)]
-    near = [c for c in ok if topo.die(c) == topo.die(core)]
-    far = [c for c in ok if topo.die(c) != topo.die(core)]
-    return near[0], far[0]
-
-
 def routes(cores, topo):
-    hp = [helpers(c, [d for d in cores if d != c], topo) for c in cores]
-    far = [[(q + 2) % N, (q + 4) % N] for q in range(N)]
-
-    def cost(sel):
-        load = {}
-        for q in range(N):
-            for r in range(N):
-                if r != q:
-                    s = hp[q][1] if r in sel[q] else cores[q]
-                    for k in links(s, cores[r], topo):
-                        load[k] = load.get(k, 0) + 1
-        return (max(load.values()), sum(v * v for v in load.values()))
-
-    best = cost(far)
-    moved = True
-    while moved:
-        moved = False
-        for q in range(N):
-            for a in range(N):
-                for b in range(a + 1, N):
-                    if q in (a, b):
-                        continue
-                    for q2 in range(N):
-                        for a2 in range(N):
-                            for b2 in range(a2 + 1, N):
-                                if q2 in (a2, b2) or (q2 == q and (a2, b2) != (a, b)) or q2 < q:
-                                    continue
-                                t = [list(f) for f in far]
-                                t[q], t[q2] = [a, b], [a2, b2]
-                                c = cost(t)
-                                if c < best:
-                                    best, far, moved = c, t, True
-    near = [[r for r in range(N) if r != q and r not in far[q]] for q in range(N)]
-    pick = None
-    for n in range(3 ** N):
-        ch = [near[q][n // 3 ** q % 3] for q in range(N)]
-        if pick is None or len(set(ch)) > len(set(pick)):
-            pick = ch
-    return [(hp[q][0], hp[q][1], pick[q], [r for r in near[q] if r != pick[q]], far[q]) for q in range(N)]
+    chips = [topo.chip(c) for c in cores]
+    pairs = [(a, b) for a in range(N) for b in range(a + 1, N) if topo.mates(chips[a], chips[b])]
+    rest = [a for a in range(N) if all(a not in p for p in pairs)]
+    pairs += [(rest[i], rest[i + 1]) for i in range(0, len(rest), 2)]
+    slot = {q: (k, s) for k in range(NP) for s, q in enumerate(pairs[k])}
+    direct = {q: list(pairs[(slot[q][0] + 1) % NP]) for q in range(N)}
+    far = {q: [r for r in range(N) if r != q and r not in direct[q]] for q in range(N)}
+    near = {q: [] for q in range(N)}
+    stages = {q: [] for q in range(N)}
+    for r in rest:
+        k, s = slot[r]
+        mate = [c for c in range(topo.CHIPS * topo.CORES_PER_CHIP) if topo.mates(topo.chip(c), chips[r])]
+        q = [q for q in range(N) if r in direct[q] and topo.same_plane(chips[q], topo.chip(mate[0]))][0]
+        direct[q].remove(r)
+        ok = [c for c in mate if topo.may_write(c, cores[r])]
+        stages[q].append(([ok[0], ok[-1]], [r]))
+        far[pairs[k][1 - s]].remove(r)
+        near[pairs[k][1 - s]].append(r)
+    for q in range(N):
+        for dsts, same in ((far[q], False), (near[q], True)):
+            if dsts:
+                ok = [c for c in topo.cores_of(cores[q]) if c != cores[q] and (topo.die(c) == topo.die(cores[q])) == same
+                      and all(topo.may_write(c, cores[r]) for r in dsts)]
+                stages[q].append((ok[:2], dsts))
+    return pairs, slot, direct, stages
 
 
 _CACHE = {}
@@ -145,51 +109,60 @@ def plan(T, topo):
     return _CACHE["r"]
 
 
+def carrier(stage, piece):
+    return stage[0][-1] if piece in "CD" else stage[0][0]
+
+
 def dst_id(c, topo):
     rid, pid, _ = topo.addr(c)
     return DstId(rid=rid, pnc=pid)
 
 
-def u8(v):
-    return v.bitcast(dt.uint8)
+def piece_view(T, slot, q, piece):
+    k, s = slot[q]
+    a, b = S1 * k, S2 * k
+    if piece == "A":
+        return T.c1[:, a + 2 * CH + SH * s:a + 2 * CH + SH * (s + 1)].bitcast(dt.uint8)
+    if piece == "B":
+        lo = a + (2 * CH + 2 * SH if s else CH)
+        return T.c1[:, lo:lo + CH].bitcast(dt.uint8)
+    if piece == "C":
+        lo = a + CH + (SH + CH) * s
+        return T.p1[:, lo:lo + SH + CH]
+    if piece == "D":
+        return T.c2[:, b + 2 * CH * s:b + 2 * CH * (s + 1)].bitcast(dt.uint8)
+    return T.p2[:, b + 2 * CH * s:b + 2 * CH * (s + 1)]
 
 
-def helper_program(g, core, T, topo, q, ranks):
-    dst = [T.cores[r] for r in ranks]
-    ids = [dst_id(c, topo) for c in dst]
+def helper_program(g, core, T, topo, slot, q, stage):
+    dst = [T.cores[r] for r in stage[1]]
     eng = [e for e in topo.engines(core, dst[0]) if all(e in topo.engines(core, d) for d in dst)]
-    wc, dc = slice(SH * q, SH * (q + 1)), slice(3 * CH * q, 3 * CH * (q + 1))
     n = 0
-    for arr, src, out, sem in ((T.sem.hwc, u8(T.hw[:]), u8(T.wl[:, wc]), "w%d" % q),
-                               (T.sem.hwp, T.hws[:], T.ws[:, wc], "w%d" % q),
-                               (T.sem.hdc, u8(T.hd[:]), u8(T.dq[:, dc]), "d%d" % q),
-                               (T.sem.hdp, T.hds[:], T.dp[:, dc], "d%d" % q)):
-        g.wait_ge(arr, 8)
-        g.remote_dma_fused([RemoteDMATransfer(dst_ids=ids, dma_engine_mask=bits(eng), remote_sem=T.sem[sem],
-                                              srcs=[src], dsts=[out for _ in dst])], local_sem=T.sem.loc)
-        n += len(eng)
+    for piece in PIECES:
+        if carrier(stage, piece) == core:
+            s, view = T.sem["a%s%d" % (piece, q)], piece_view(T, slot, q, piece)
+            g.wait_ge(s, 8)
+            g.remote_dma_fused([RemoteDMATransfer(dst_ids=[dst_id(c, topo) for c in dst], dma_engine_mask=bits(eng),
+                                                  remote_sem=s, srcs=[view], dsts=[view for _ in dst])],
+                               local_sem=T.sem.loc)
+            n += len(eng)
     g.wait_ge(T.sem.loc, n)
 
 
 def rank_program(g, core, T, topo):
-    P = plan(T, topo)
+    pairs, slot, direct, stages = plan(T, topo)
     r = T.rank_of(core)
     if r is None:
         for q in range(N):
-            if core == P[q][0]:
-                helper_program(g, core, T, topo, q, P[q][3])
-            if core == P[q][1]:
-                helper_program(g, core, T, topo, q, P[q][4])
+            for stage in stages[q]:
+                if core in stage[0]:
+                    helper_program(g, core, T, topo, slot, q, stage)
         return
-    near, far, direct, _, _ = P[r]
-    odd = r % 2
-    mcol = 0 if odd else 512
-    dcol = [None] + [(320 + CH * (k - 1)) if odd else (320 - CH * k) for k in (1, 2, 3)]
-    dlow = 320 if odd else 128
-    gap = (128, 320) if odd else (320, 512)
-    org = [None, mcol, 0 if odd else dcol[1], 0 if odd else dcol[2]]
-    end = [None, mcol + SH, dcol[1] + CH if odd else WIN, dcol[2] + CH if odd else WIN]
+    own, odd = slot[r]
+    wcol = 0 if odd else 3 * CH
+    dcol = [None] + [(SH + CH * (k - 1)) if odd else CH * (3 - k) for k in (1, 2, 3)]
     add, mult = AluOpType.add, AluOpType.mult
+    band, shr = AluOpType.bitwise_and, AluOpType.arith_shift_right
     cnt = {"v": 0, "s": 0, "p": 0, "g": 0}
     sem = {"v": T.sem.vs, "s": T.sem.ss, "p": T.sem.ps, "g": T.sem.gs}
     queue = {"v": g.vector, "s": g.scalar, "p": g.tensor, "g": g, "y": g.sync}
@@ -207,141 +180,167 @@ def rank_program(g, core, T, topo):
             queue[on].wait_ge(sem[s] if s in sem else T.sem[s], val)
 
     v, sc, y, te = g.vector, g.scalar, g.sync, g.tensor
-    wc, dc = slice(SH * r, SH * (r + 1)), slice(3 * CH * r, 3 * CH * (r + 1))
+    Copy, Ident = ActivationFunctionType.Copy, ActivationFunctionType.Identity
 
+    y.dma_start(T.md[:, 4 * wcol:4 * wcol + 4 * SH], T.wm[:]).then_inc(T.sem.lwm, 16)
     for k in range(4):
         y.dma_start(T.ix[16 * k:16 * k + 16, :], T.idx[:]).then_inc(T.sem.lix, 16)
         sc.dma_start(T.ix[64 + 16 * k:64 + 16 * k + 16, :], T.idx[:]).then_inc(T.sem.lix, 16)
-    y.dma_start(T.md[:, 4 * mcol:4 * mcol + 512], T.wm[:]).then_inc(T.sem.lwm, 16)
-    sc.dma_start(T.dlt[:], T.dl[:]).then_inc(T.sem.ldl, 16)
-    y.dma_start(T.xt[:], T.x[:]).then_inc(T.sem.lx, 16)
+    y.dma_start(T.dlt[:, 0:4 * CH], T.dl[:, 0:4 * CH]).then_inc(T.sem.ld1, 16)
+    sc.dma_start(T.dlt[:, 4 * CH:12 * CH], T.dl[:, 4 * CH:12 * CH]).then_inc(T.sem.ld2, 16)
+    sc.dma_start(T.xt[:], T.x[:]).then_inc(T.sem.lx, 16)
 
+    small = {"allow_small_or_imprecise_dtypes": True}
     g_pi = done("g", g.iota(T.pi[:], [[0, 1]], 0, 1))
-    g_mi = done("g", g.iota(T.mi[:], [[-4, CH]], 4 * CH, 1))
-    g_lw = done("g", g.iota(T.lw[:], [[1, 16], [0, 3], [16, 8]], mcol, 0, allow_small_or_imprecise_dtypes=True))
-    g_vl = done("g", g.iota(T.vl[:], [[CH if odd else -CH, 3], [1, CH]], dcol[1], 0, allow_small_or_imprecise_dtypes=True))
-    g_rm = done("g", g.iota(T.rm[:], [[0, 16], [1024, 4]], 0, 0, allow_small_or_imprecise_dtypes=True))
+    done("g", g.iota(T.mi[:, 128:176], [[1, 48]], 128, -1))
+    g_mi = done("g", g.iota(T.mi[:, 0:128], [[4, 128]], 512 + 3, -1))
+    g_jj = done("g", g.iota(T.jj[:], [[16, 3]], 0, 48))
+    done("g", g.iota(T.tb[:, 0:SH], [[1, SH]], CH + SH * odd, 0, **small))
+    g_vl = done("g", g.iota(T.vl[:], [[2 * CH * odd, 3], [1, CH]], (CH + 2 * SH) * odd, 0, **small))
 
-    done("v", v.memset(T.md[:, 4 * gap[0]:4 * gap[1]], 0.0))
+    done("v", v.memset(T.md[:, 4 * dcol[2]:4 * dcol[2] + 4 * CH], 0.0))
+    wait("v", "g", g_pi)
+    done("v", v.tensor_scalar(T.pa[:], T.pi[:], 3, None, shr))
+    a = done("v", v.tensor_scalar(T.pe[:], T.pi[:], 3, None, band))
+    wait("v", "v", a)
+    done("v", v.tensor_scalar(T.pf[:], T.pa[:], -383, None, mult))
     wait("v", "g", g_mi)
-    v_pe = done("v", v.tensor_scalar(T.pe[:], T.pi[:], 3, None, AluOpType.bitwise_and))
-    v_mj = done("v", v.tensor_scalar(T.mj[:], T.mi[:], 2, 3, AluOpType.arith_shift_right, AluOpType.bitwise_and))
-    wait("v", "v", v_pe)
-    for k in (1, 2, 3):
-        done("v", v.tensor_scalar(T["e%d" % k][:], T.pe[:], -4 * org[k], None, add))
-    wait("v", "v", v_mj)
-    done("v", v.tensor_scalar(T.mk[:], T.mj[:], 0, None, AluOpType.is_equal))
-    wait("v", "lix", 128)
-    v_lo = done("v", v.tensor_scalar(T.lo[:], T.ix[:], 15, None, AluOpType.bitwise_and))
-    done("v", v.tensor_scalar(T.hi[:], T.ix[:], 4, None, AluOpType.arith_shift_right))
-    wait("v", "v", v_lo)
-    a = done("v", v.tensor_scalar(T.lm[:], T.lo[:], 24, None, mult))
+    done("v", v.tensor_scalar(T.mj[:, 128:176], T.mi[:, 128:176], 15, None, band))
+    a = done("v", v.tensor_scalar(T.mj[:, 0:128], T.mi[:, 0:128], 2, 3, shr, band))
     wait("v", "v", a)
-    a = done("v", v.tensor_tensor(T.sm[:], T.lm[:], T.hi[:], add))
+    done("v", v.tensor_scalar(T.ma[:], T.mj[:], 0, 3 * BIG, AluOpType.is_equal, mult))
+    a = done("v", v.tensor_scalar(T.mb[:], T.mj[:], 1, -BIG, AluOpType.is_equal, mult))
+    wait("v", "g", g_jj)
+    v_co = done("v", v.tensor_scalar(T.co[:, 0:3], T.jj[:], T.pf[:], None, add))
     wait("v", "v", a)
-    done("v", v.tensor_copy(T.piu[:], T.sm[:]))
+    done("v", v.tensor_scalar(T.lc[:], T.ma[:, 143:144], 1, BIG, AluOpType.is_lt, mult))
+    a = done("v", v.tensor_scalar(T.ec[:], T.ma[:, 3:4], 1, 4 * BIG, AluOpType.is_lt, mult))
+    done("v", v.tensor_tensor(T.cs[:], T.ma[:], T.mb[:], add))
+    wait("v", "v", a)
+    done("v", v.tensor_scalar(T.e2[:], T.pe[:], T.ec[:], -4 * 3 * CH * odd, add, add))
+    done("v", v.tensor_scalar(T.e3[:], T.pe[:], T.ec[:], -4 * 4 * CH * odd, add, add))
 
-    def place(k, t):
-        wait("v", "v", cnt["v"])
-        return done("v", v.tensor_copy(T.lw[:, 8 * (t - 1):3 * SH].indirect(T.piu[:, 4 * (k - 1):4 * k]),
-                                       T.vl[:, CH * (k - 1):CH * k]))
-
-    def look(t, k):
-        wait("v", "v", cnt["v"])
-        return done("v", v.tensor_tensor(T["k%d" % k][:], T.lw[:, 8 * (t - 1):3 * SH].indirect(T.piu[:, 4 * (k - 1):4 * k]),
-                                         T.mk[:], mult))
-
-    wait("v", "g", g_rm)
-    look(3, 1)
-    place(1, 1)
-    look(1, 2)
+    a1, a2 = S1 * own, S2 * own
+    wq = slice(a1 + 2 * CH + SH * odd, a1 + 2 * CH + SH * (odd + 1))
     wait("v", "lwm", 16)
-    v_qw = done("v", v.quantize_mx(T.wl[:, wc], T.ws[:, wc], T.md[:, 4 * mcol:4 * mcol + 512]))
-    place(1, 2)
-    place(2, 2)
-    look(2, 3)
-    place(1, 3)
-    place(2, 3)
-    place(3, 3)
-    wait("v", "v", cnt["v"])
-    v_lu = done("v", v.tensor_copy(T.lu[0:1, :], T.lw[0:1, :]))
-    scan = {}
-    for k in (1, 2, 3):
-        scan[k] = done("v", v.tensor_tensor_scan(T["c%d" % k][:], T.rm[:], T["k%d" % k][:], 0.0, AluOpType.min, add))
-    for k in (1, 2, 3):
-        wait("v", "v", scan[k])
-        done("v", v.tensor_scalar(T["o%d" % k][:], T["c%d" % k][:, 3:CH:4], 4, T["e%d" % k][:], mult, add))
-    for k in (1, 2, 3):
-        wait("v", "v", cnt["v"])
-        wait("v", "s", k)
-        done("v", v.tensor_tensor(T.md[:, 4 * dcol[k]:4 * dcol[k] + 4 * CH],
-                                  T.md[:, 4 * org[k]:4 * end[k]].indirect(T["o%d" % k][:]),
+    v_qw = done("v", v.quantize_mx(T.c1[:, wq], T.p1[:, wq], T.md[:, 4 * wcol:4 * wcol + 4 * SH]))
+    wait("v", "lix", 128)
+    a = done("v", v.tensor_copy(T.o1[:], T.ix[:]))
+    v_o4 = done("v", v.tensor_scalar(T.o4[:], T.ix[:, 0:4], 4, None, mult))
+
+    def scale(k, s):
+        wait("s", s, 16)
+        sl = slice(4 * CH * (k - 1), 4 * CH * k)
+        return done("s", sc.activation(T.dls[:, sl], T.dlt[:, sl], Copy, scale=0.25))
+
+    def table(t):
+        return T.tb[:, SH * (t - 1):SH * t]
+
+    def place(t):
+        return done("v", v.tensor_copy(table(t).indirect(T.o1[:, 4 * (t - 1):4 * t]), T.vl[:, CH * (t - 1):CH * t]))
+
+    def carry(t, after):
+        wait("s", "v", after)
+        a = done("s", sc.activation(table(t + 1), table(t), Ident, bias=float(CH)))
+        b = done("s", sc.activation(T.lk[:, CH * (t - 1):CH * t], table(t).indirect(T.o1[:, 4 * t:4 * t + 4]), Copy))
+        return a, b
+
+    def first(e):
+        return done("v", v.tensor_tensor(T.md[:, 4 * dcol[1] + e:4 * dcol[1] + 4 * CH:4],
+                                         T.md[:, 4 * wcol + e:4 * wcol + 4 * SH].indirect(T.o4[:]),
+                                         T.dls[:, e:4 * CH:4], add))
+
+    s_d1 = scale(1, "ld1")
+    wait("v", "v", a)
+    wait("v", "g", g_vl)
+    a = place(1)
+    s_t2, _ = carry(1, a)
+    s_d2 = scale(2, "ld2")
+    wait("v", "v", v_o4)
+    wait("v", "s", s_d1)
+    first(0)
+    first(1)
+    wait("v", "s", s_t2)
+    a = place(2)
+    s_t3, _ = carry(2, a)
+    first(2)
+    v_d1 = first(3)
+    wait("v", "s", s_t3)
+    a = place(3)
+    wait("s", "v", a)
+    s_lk = done("s", sc.activation(T.lk[:, 128:176], T.tb[:].indirect(T.co[:, 0:3]), Copy))
+    s_d3 = scale(3, "ld2")
+    q1 = slice(a1 + (S1 - 2 * CH) * odd, a1 + (S1 - 2 * CH) * odd + 2 * CH)
+    m1 = min(dcol[1], dcol[2])
+    wait("v", "v", v_d1)
+    v_q1 = done("v", v.quantize_mx(T.c1[:, q1], T.p1[:, q1], T.md[:, 4 * m1:4 * m1 + 8 * CH]))
+    wait("v", "s", s_lk)
+    a = done("v", v.tensor_tensor_scan(T.sn[:], T.cs[:], T.lk[:], 0.0, add, AluOpType.min))
+    wait("v", "v", a)
+    v_ls = done("v", v.tensor_scalar(T.ls[:], T.sn[:, 143:176:16], T.lc[:], None, add))
+    done("v", v.tensor_scalar(T.o2[:], T.sn[:, 3:CH:4], 4, T.e2[:], mult, add))
+    done("v", v.tensor_scalar(T.o3[:], T.sn[:, CH + 3:2 * CH:4], 4, T.e3[:], mult, add))
+    for k, s in ((2, s_d2), (3, s_d3)):
+        lo, hi = (0, dcol[k]) if odd else (dcol[k] + CH, SH + 3 * CH)
+        wait("v", "v", cnt["v"] - (3 - k))
+        wait("v", "s", s)
+        done("v", v.tensor_tensor(T.md[:, 4 * dcol[k]:4 * dcol[k] + 4 * CH], T.md[:, 4 * lo:4 * hi].indirect(T["o%d" % k][:]),
                                   T.dls[:, 4 * CH * (k - 1):4 * CH * k], add))
+    q2 = slice(a2 + 2 * CH * odd, a2 + 2 * CH * (odd + 1))
+    m2 = min(dcol[2], dcol[3])
     wait("v", "v", cnt["v"])
-    v_qd = done("v", v.quantize_mx(T.dq[:, dc], T.dp[:, dc], T.md[:, 4 * dlow:4 * dlow + 12 * CH]))
+    v_q2 = done("v", v.quantize_mx(T.c2[:, q2], T.p2[:, q2], T.md[:, 4 * m2:4 * m2 + 8 * CH]))
     wait("v", "lx", 16)
     v_qx = done("v", v.quantize_mx(T.xq[:], T.xs[:], T.xt[:]))
-    for p in range(NP):
-        for t in (1, 2):
-            for lo, hi in ((128, 320 - CH * t), (320 + CH * t, 512)):
-                v_ms = done("v", v.memset(T["pw%d" % t][:, WIN * p + lo:WIN * p + hi], 0.0))
 
-    wait("s", "ldl", 16)
-    for k in range(3):
-        sl = slice(4 * CH * k, 4 * CH * (k + 1))
-        done("s", sc.activation(T.dls[:, sl], T.dlt[:, sl], ActivationFunctionType.Copy, scale=0.25))
-
-    onchip = topo.engines(core, far)
-    ef, en = onchip[0::2], onchip[1::2]
-    drk = T.cores[direct]
-    ed = topo.engines(core, drk)
+    others = [T.cores[q] for q in range(N) if q != r]
+    out = topo.engines(core, others[0])
     nloc = [0]
 
-    def hand(src, out, s):
-        g.remote_dma_fused([RemoteDMATransfer(dst_ids=[dst_id(far, topo)], dma_engine_mask=bits(ef), remote_sem=T.sem[s],
-                                              srcs=[src], dsts=[out]),
-                            RemoteDMATransfer(dst_ids=[dst_id(near, topo)], dma_engine_mask=bits(en), remote_sem=T.sem[s],
-                                              srcs=[src], dsts=[out])], local_sem=T.sem.loc)
-        nloc[0] += len(ef) + len(en)
+    def send(piece):
+        view = piece_view(T, slot, r, piece)
+        dst = [T.cores[q] for q in direct[r]] + [carrier(stage, piece) for stage in stages[r]]
+        off = [c for c in dst if topo.chip(c) != topo.chip(core)]
+        on = [c for c in dst if topo.chip(c) == topo.chip(core)]
+        rest = [e for e in topo.engines(core, on[0]) if e not in out]
+        g.remote_dma_fused([RemoteDMATransfer(dst_ids=[dst_id(c, topo) for c in d], dma_engine_mask=bits(e),
+                                              remote_sem=T.sem["a%s%d" % (piece, r)], srcs=[view], dsts=[view for _ in d])
+                            for d, e in ((on, rest), (off, out))], local_sem=T.sem.loc)
+        nloc[0] += len(rest) + len(out)
 
-    def send(view, s):
-        g.remote_dma_fused([RemoteDMATransfer(dst_ids=[dst_id(drk, topo)], dma_engine_mask=bits(ed), remote_sem=T.sem[s],
-                                              srcs=[view], dsts=[view])], local_sem=T.sem.loc)
-        nloc[0] += len(ed)
-
-    wait("g", "v", v_qw)
-    hand(u8(T.wl[:, wc]), u8(T.hw[:]), "hwc")
-    hand(T.ws[:, wc], T.hws[:], "hwp")
-    send(u8(T.wl[:, wc]), "w%d" % r)
-    send(T.ws[:, wc], "w%d" % r)
-    others = [T.cores[q] for q in range(N) if q != r]
     land = T.lland[128 * r:128 * (r + 1), :]
-    wait("g", "lbo", 16)
-    g.remote_dma_fused([RemoteDMATransfer(dst_ids=[dst_id(c, topo) for c in others], dma_engine_mask=bits(ed[:1]),
-                                          remote_sem=T.sem.lst, srcs=[T.lsend[:]], dsts=[land for _ in others])],
+    wait("g", "v", v_qw)
+    send("A")
+    wait("g", "v", v_q1)
+    send("B")
+    send("C")
+    wait("g", "v", v_ls)
+    g.remote_dma_fused([RemoteDMATransfer(dst_ids=[dst_id(c, topo) for c in others], dma_engine_mask=bits(out),
+                                          remote_sem=T.sem.lst, srcs=[T.ls[:]], dsts=[land for _ in others])],
                        local_sem=T.sem.loc)
-    nloc[0] += 1
-    wait("g", "v", v_qd)
-    hand(u8(T.dq[:, dc]), u8(T.hd[:]), "hdc")
-    hand(T.dp[:, dc], T.hds[:], "hdp")
-    send(u8(T.dq[:, dc]), "d%d" % r)
-    send(T.dp[:, dc], "d%d" % r)
+    nloc[0] += len(out)
+    wait("g", "v", v_q2)
+    send("D")
+    send("E")
 
-    wait("y", "v", v_lu)
-    y.dma_start(T.lsend[:], T.lu[0:1, :]).then_inc(T.sem.lbo, 16)
+    def lay(q):
+        c = 16 * slot[q][0] + 8 * slot[q][1]
+        for h in range(2):
+            y.dma_start(T.offs[16 * h:16 * h + 16, :, c:c + 8], T.lland[128 * q:128 * (q + 1), :]).then_inc(T.sem.st2, 16)
+
+    wait("y", "v", v_ls)
+    y.dma_start(land, T.ls[:]).then_inc(T.sem.lbo, 16)
     wait("y", "lbo", 16)
-    y.dma_start(T.comb[:, :, 8 * r:8 * r + 8], T.lsend[:]).then_inc(T.sem.st1, 16)
-    wait("y", "lst", N - 1)
+    lay(r)
+    wait("y", "lst", len(out) * (N - 1))
     for q in range(N):
         if q != r:
-            y.dma_start(T.comb[:, :, 8 * q:8 * q + 8], T.lland[128 * q:128 * (q + 1), :]).then_inc(T.sem.st1, 16)
-    wait("y", "st1", 16 * N)
-    for k in range(8):
-        y.dma_start(T.offs[16 * k:16 * k + 16, :], T.comb[:]).then_inc(T.sem.st2, 16)
+            lay(q)
 
-    order = [(r // 2 + k) % NP for k in range(NP)]
-    units = [("w", p, t) for p in order for t in range(RD)] + [("d", p, t) for p in order for t in (1, 3, 2)]
-    eng = {u: (("s" if u[2] in (0, 2) else "v") if u[0] == "w" else ("v" if u[2] == 3 else "s")) for u in units}
+    A, B, C = own, (own - 1) % NP, (own + 1) % NP
+    order = (B, A, C)
+    units = [(1, p, t) for p in order for t in (1, 0, 3, 2)] + [(2, p, t) for p in order for t in (3, 2)]
+    eng = {u: "v" if u[2] % 2 else "s" for u in units}
     bank, use = {}, {"v": 0, "s": 0}
     for u in units:
         e = eng[u]
@@ -353,84 +352,81 @@ def rank_program(g, core, T, topo):
         return T.pb[:, 512 * bank[u] + lo:512 * bank[u] + hi]
 
     def copy(e, out, in_):
-        return done(e, v.tensor_copy(out, in_) if e == "v" else sc.activation(out, in_, ActivationFunctionType.Copy))
+        return done(e, v.tensor_copy(out, in_) if e == "v" else sc.activation(out, in_, Copy))
 
-    drained, got, shard = {}, {}, {}
+    drained, got, spread = {}, {}, [0]
 
-    def drain(e, u):
-        kind, p, t = u
+    def drain(*u):
+        ph, p, t = u
+        e = eng[u]
         wait(e, "p", num[u])
-        if kind == "w" and t == 0:
+        if t == 0:
             drained[u] = copy(e, T.y0[:, 256 * p:256 * p + 256], ps(u, 0, 256))
-        elif kind == "w":
-            copy(e, T["pw%d" % t][:, WIN * p + 512:WIN * p + 640], ps(u, 0, 128))
-            drained[u] = copy(e, T["pw%d" % t][:, WIN * p:WIN * p + 128], ps(u, 128, 256))
-            shard[(p, t)] = (e, drained[u])
+            got[(p, 0)] = (e, drained[u])
+            return
+        pw, lo, n = T["pw%d" % t], win(t) * p, CH * (t - 1)
+        if ph == 1:
+            drained[u] = copy(e, pw[:, lo + n:lo + n + win(1)], ps(u, 0, win(1)))
         else:
-            drained[u] = copy(e, T["pw%d" % t][:, WIN * p + 320 - CH * t:WIN * p + 320 + CH * t], ps(u, 0, 128 * t))
+            copy(e, pw[:, lo:lo + n], ps(u, 0, n))
+            drained[u] = copy(e, pw[:, lo + win(t) - n:lo + win(t)], ps(u, n, 2 * n))
 
     def gather(e, p, t):
-        wait(e, "st2", 128)
-        wait(e, "v", v_ms)
-        wait(e, shard[(p, t)][0], shard[(p, t)][1])
-        wait(e, eng[("d", p, t)], drained[("d", p, t)])
-        win = T["pw%d" % t][:, WIN * p:WIN * p + WIN].indirect(T.offs[:, 48 * (t - 1) + 16 * p:48 * (t - 1) + 16 * p + 16])
-        got[(p, t)] = (e, copy(e, T["y%d" % t][:, 256 * p:256 * p + 256], win))
+        wait(e, "v", spread[0])
+        u = (1 if t == 1 else 2, p, t)
+        wait(e, eng[u], drained[u])
+        window = T["pw%d" % t][:, win(t) * p:win(t) * (p + 1)].indirect(T.offs[:, t - 1, 16 * p:16 * p + 16])
+        got[(p, t)] = (e, copy(e, T["y%d" % t][:, 256 * p:256 * p + 256], window))
 
+    for p in (B, A):
+        for t in (1, 0, 3, 2):
+            drain(1, p, t)
+    wait("v", "st2", 32 * N)
+    for k in (1, 2, 3):
+        spread[0] = done("v", v.tensor_copy(T.offs[32 * k:32 * k + 32, :, :], T.offs[0:32, :, :]))
+    gather("v", B, 1)
+    for t in (1, 0, 3, 2):
+        drain(1, C, t)
+    gather("s", A, 1)
+    gather("s", C, 1)
     for p in order:
-        drain("s", ("w", p, 0))
-        drain("s", ("w", p, 2))
-        wait("s", "s", drained[("w", p, 0)])
-        sc.dma_start(T.y[:, 256 * p:256 * p + 256], T.y0[:, 256 * p:256 * p + 256]).then_inc(T.sem.sty, 16)
-        drain("v", ("w", p, 1))
-        drain("v", ("w", p, 3))
-    A, B, C = order
-    for p in (A, B):
-        drain("s", ("d", p, 1))
-        drain("s", ("d", p, 2))
-        drain("v", ("d", p, 3))
-    gather("v", A, 1)
-    gather("v", A, 3)
-    gather("s", A, 2)
-    gather("v", B, 3)
-    gather("s", B, 1)
-    gather("s", B, 2)
-    drain("s", ("d", C, 1))
-    drain("s", ("d", C, 2))
-    drain("v", ("d", C, 3))
-    gather("s", C, 2)
-    gather("v", C, 1)
-    gather("v", C, 3)
+        for t in (3, 2):
+            drain(2, p, t)
+            gather(eng[(2, p, t)], p, t)
 
     wait("p", "v", v_qx)
     last = {}
     for u in units:
-        kind, p, t = u
-        for q in (2 * p, 2 * p + 1):
+        ph, p, t = u
+        for q in pairs[p]:
             if q != r:
-                wait("p", ("w%d" if kind == "w" else "d%d") % q, 16)
+                for piece in ("ABC" if ph == 1 else "DE"):
+                    wait("p", "a%s%d" % (piece, q), 8)
         b = bank[u]
         if b in last:
             wait("p", eng[u], drained[last[b]])
         last[b] = u
-        if kind == "w":
-            n, lo = 256, 256 * p
-            codes, scales = T.wl, T.ws
+        if ph == 1:
+            n = 2 * SH if t == 0 else win(1)
+            lo, codes, scales = S1 * p + (S1 - n) // 2, T.c1, T.p1
         else:
-            n, lo = 128 * t, 384 * p + 192 - CH * t
-            codes, scales = T.dq, T.dp
+            n = 2 * CH * (t - 1)
+            lo, codes, scales = S2 * p + (S2 - n) // 2, T.c2, T.p2
         done("p", te.matmul_mx(ps(u, 0, n), T.xq[:, 128 * t:128 * t + 128], T.xs[:, 128 * t:128 * t + 128],
                                codes[:, lo:lo + n], scales[:, lo:lo + n], True, True))
 
-    for p, t in ((A, 1), (A, 2), (A, 3), (B, 1), (B, 3), (B, 2), (C, 1), (C, 2), (C, 3)):
+    stores = 0
+    for p, t in [(B, 0), (A, 0), (B, 1), (C, 0), (A, 1), (C, 1)] + [(p, t) for p in order for t in (2, 3)]:
         e, k = got[(p, t)]
         wait("y", e, k)
-        y.dma_start(T.y[:, SH * N * t + 256 * p:SH * N * t + 256 * p + 256],
-                    T["y%d" % t][:, 256 * p:256 * p + 256]).then_inc(T.sem.stz, 16)
+        a, b = pairs[p]
+        runs = [(a, 0, 2 * SH)] if b == a + 1 else [(a, 0, SH), (b, SH, SH)]
+        for q, lo, n in runs:
+            y.dma_start(T.y[:, SH * (N * t + q):SH * (N * t + q) + n],
+                        T["y%d" % t][:, 256 * p + lo:256 * p + lo + n]).then_inc(T.sem.stz, 16)
+            stores += 1
 
     wait("g", "loc", nloc[0])
     for k in ("g", "v", "s", "p"):
         wait("g", k, cnt[k])
-    wait("g", "st2", 128)
-    wait("g", "sty", 16 * NP)
-    wait("g", "stz", 16 * 3 * NP)
+    wait("g", "stz", 16 * stores)

@@ -6,8 +6,10 @@ N, SH, CH, RD = 6, 128, 64, 4
 NP = N // 2
 S1, S2 = 2 * SH + 4 * CH, 4 * CH
 BIG = 1024.0
+LK = 2 * CH + 48
 F8 = "float8_e4m3fn_x4"
-PIECES = "ABCDE"
+PIECES = "ABCDEF"
+PHASE = {"w": "AB", "u": "CD", "e": "EF"}
 
 
 def win(t):
@@ -38,17 +40,17 @@ SCRATCH = {
     "ec": ("sbuf", [128, 1], "float32"),
     "e2": ("sbuf", [128, 1], "float32"),
     "e3": ("sbuf", [128, 1], "float32"),
-    "jj": ("sbuf", [128, 3], "int32"),
+    "jj": ("sbuf", [128, 4], "int32"),
     "co": ("sbuf", [128, 4], "uint16"),
-    "mi": ("sbuf", [128, 176], "int32"),
-    "mj": ("sbuf", [128, 176], "int32"),
-    "ma": ("sbuf", [128, 176], "float32"),
-    "mb": ("sbuf", [128, 176], "float32"),
-    "cs": ("sbuf", [128, 176], "float32"),
+    "mi": ("sbuf", [128, 32], "int32"),
+    "mj": ("sbuf", [128, 32], "int32"),
+    "ma": ("sbuf", [128, 32], "float32"),
+    "mb": ("sbuf", [128, 32], "float32"),
+    "cs": ("sbuf", [128, LK], "float32"),
     "vl": ("sbuf", [128, 3 * CH], "float32"),
     "tb": ("sbuf", [128, 3 * SH], "float32"),
-    "lk": ("sbuf", [128, 176], "float32"),
-    "sn": ("sbuf", [128, 176], "float32"),
+    "lk": ("sbuf", [128, LK], "float32"),
+    "sn": ("sbuf", [128, LK], "float32"),
     "ls": ("sbuf", [128, 3], "uint16"),
     "lland": ("dram", [N * 128, 3], "uint16"),
     "offs": ("sbuf", [128, 3, 8 * N], "uint16"),
@@ -61,7 +63,7 @@ SCRATCH = {
     "y3": ("sbuf", [128, N * SH], "float32"),
     "pb": ("psum", [128, 512 * 8], "float32"),
 }
-SEMAPHORES = (["vs", "ss", "ps", "gs", "lix", "lwm", "ld1", "ld2", "lx", "lbo", "st2", "stz", "loc", "lst"]
+SEMAPHORES = (["vs", "ss", "ps", "gs", "lix", "lwm", "ld1", "ld2", "lx", "lbo", "st2", "stz", "loc"] + ["l%d" % q for q in range(N)]
               + ["a%s%d" % (p, q) for p in PIECES for q in range(N)])
 
 
@@ -89,8 +91,10 @@ def routes(cores, topo):
         direct[q].remove(r)
         ok = [c for c in mate if topo.may_write(c, cores[r])]
         stages[q].append(([ok[0], ok[-1]], [r]))
-        far[pairs[k][1 - s]].remove(r)
-        near[pairs[k][1 - s]].append(r)
+    for a, b in pairs:
+        for q, r in ((a, b), (b, a)):
+            far[q].remove(r)
+            near[q].append(r)
     for q in range(N):
         for dsts, same in ((far[q], False), (near[q], True)):
             if dsts:
@@ -110,7 +114,7 @@ def plan(T, topo):
 
 
 def carrier(stage, piece):
-    return stage[0][-1] if piece in "CD" else stage[0][0]
+    return stage[0][0] if piece in "ACF" else stage[0][-1]
 
 
 def dst_id(c, topo):
@@ -118,20 +122,22 @@ def dst_id(c, topo):
     return DstId(rid=rid, pnc=pid)
 
 
-def piece_view(T, slot, q, piece):
+def columns(slot, q, phase):
     k, s = slot[q]
-    a, b = S1 * k, S2 * k
-    if piece == "A":
-        return T.c1[:, a + 2 * CH + SH * s:a + 2 * CH + SH * (s + 1)].bitcast(dt.uint8)
-    if piece == "B":
-        lo = a + (2 * CH + 2 * SH if s else CH)
-        return T.c1[:, lo:lo + CH].bitcast(dt.uint8)
-    if piece == "C":
-        lo = a + CH + (SH + CH) * s
-        return T.p1[:, lo:lo + SH + CH]
-    if piece == "D":
-        return T.c2[:, b + 2 * CH * s:b + 2 * CH * (s + 1)].bitcast(dt.uint8)
-    return T.p2[:, b + 2 * CH * s:b + 2 * CH * (s + 1)]
+    if phase == "w":
+        return S1 * k + 2 * CH + SH * s, SH
+    if phase == "d":
+        return S1 * k + (2 * CH + 2 * SH if s else CH), CH
+    if phase == "u":
+        return S1 * k + CH + (SH + CH) * s, SH + CH
+    return S2 * k + 2 * CH * s, 2 * CH
+
+
+def piece_view(T, slot, q, piece):
+    lo, n = columns(slot, q, "wwddee"[PIECES.index(piece)])
+    if piece in "ACE":
+        return (T.c2 if piece == "E" else T.c1)[:, lo:lo + n].bitcast(dt.uint8)
+    return (T.p2 if piece == "F" else T.p1)[:, lo:lo + n]
 
 
 def helper_program(g, core, T, topo, slot, q, stage):
@@ -192,38 +198,47 @@ def rank_program(g, core, T, topo):
 
     small = {"allow_small_or_imprecise_dtypes": True}
     g_pi = done("g", g.iota(T.pi[:], [[0, 1]], 0, 1))
-    done("g", g.iota(T.mi[:, 128:176], [[1, 48]], 128, -1))
-    g_mi = done("g", g.iota(T.mi[:, 0:128], [[4, 128]], 512 + 3, -1))
-    g_jj = done("g", g.iota(T.jj[:], [[16, 3]], 0, 48))
-    done("g", g.iota(T.tb[:, 0:SH], [[1, SH]], CH + SH * odd, 0, **small))
-    g_vl = done("g", g.iota(T.vl[:], [[2 * CH * odd, 3], [1, CH]], (CH + 2 * SH) * odd, 0, **small))
+    done("g", g.iota(T.mi[:, 16:32], [[1, 16]], 128, -1))
+    g_mi = done("g", g.iota(T.mi[:, 0:16], [[4, 16]], 512 + 3, -1))
+    g_jj = done("g", g.iota(T.jj[:, 0:3], [[16, 3]], 0, 48))
+    g_v1 = done("g", g.iota(T.vl[:, 0:CH], [[1, CH]], (CH + 2 * SH) * odd, 0, **small))
+    g_vl = done("g", g.iota(T.tb[:, 0:SH], [[1, SH]], CH + SH * odd, 0, **small))
 
     done("v", v.memset(T.md[:, 4 * dcol[2]:4 * dcol[2] + 4 * CH], 0.0))
     wait("v", "g", g_pi)
     done("v", v.tensor_scalar(T.pa[:], T.pi[:], 3, None, shr))
     a = done("v", v.tensor_scalar(T.pe[:], T.pi[:], 3, None, band))
     wait("v", "v", a)
-    done("v", v.tensor_scalar(T.pf[:], T.pa[:], -383, None, mult))
+    done("v", v.tensor_scalar(T.pf[:], T.pa[:], 1 - 3 * SH, None, mult))
     wait("v", "g", g_mi)
-    done("v", v.tensor_scalar(T.mj[:, 128:176], T.mi[:, 128:176], 15, None, band))
-    a = done("v", v.tensor_scalar(T.mj[:, 0:128], T.mi[:, 0:128], 2, 3, shr, band))
+    done("v", v.tensor_scalar(T.mj[:, 16:32], T.mi[:, 16:32], 15, None, band))
+    a = done("v", v.tensor_scalar(T.mj[:, 0:16], T.mi[:, 0:16], 2, 3, shr, band))
     wait("v", "v", a)
     done("v", v.tensor_scalar(T.ma[:], T.mj[:], 0, 3 * BIG, AluOpType.is_equal, mult))
     a = done("v", v.tensor_scalar(T.mb[:], T.mj[:], 1, -BIG, AluOpType.is_equal, mult))
     wait("v", "g", g_jj)
-    v_co = done("v", v.tensor_scalar(T.co[:, 0:3], T.jj[:], T.pf[:], None, add))
+    done("v", v.tensor_scalar(T.co[:, 0:3], T.jj[:, 0:3], T.pf[:], None, add))
     wait("v", "v", a)
-    done("v", v.tensor_scalar(T.lc[:], T.ma[:, 143:144], 1, BIG, AluOpType.is_lt, mult))
+    done("v", v.tensor_tensor(T.cs[:, 0:16], T.ma[:, 0:16], T.mb[:, 0:16], add))
+    v_cs = done("v", v.tensor_tensor(T.cs[:, 2 * CH:2 * CH + 16], T.ma[:, 16:32], T.mb[:, 16:32], add))
+    done("v", v.tensor_scalar(T.lc[:], T.ma[:, 31:32], 1, BIG, AluOpType.is_lt, mult))
     a = done("v", v.tensor_scalar(T.ec[:], T.ma[:, 3:4], 1, 4 * BIG, AluOpType.is_lt, mult))
-    done("v", v.tensor_tensor(T.cs[:], T.ma[:], T.mb[:], add))
+    wait("s", "g", g_v1)
+    for t in (1, 2):
+        done("s", sc.activation(T.vl[:, CH * t:CH * (t + 1)], T.vl[:, 0:CH], Ident, bias=float(2 * CH * t * odd)))
+    wait("s", "v", v_cs)
+    for lo, n, to in ((0, 16, 16), (2 * CH, 16, 2 * CH + 16), (2 * CH, 16, 2 * CH + 32), (0, 32, 32), (0, 64, 64)):
+        wait("s", "s", cnt["s"] - (2 if n == 32 else 0 if n == 64 else cnt["s"]))
+        done("s", sc.activation(T.cs[:, to:to + n], T.cs[:, lo:lo + n], Copy))
     wait("v", "v", a)
     done("v", v.tensor_scalar(T.e2[:], T.pe[:], T.ec[:], -4 * 3 * CH * odd, add, add))
     done("v", v.tensor_scalar(T.e3[:], T.pe[:], T.ec[:], -4 * 4 * CH * odd, add, add))
 
-    a1, a2 = S1 * own, S2 * own
-    wq = slice(a1 + 2 * CH + SH * odd, a1 + 2 * CH + SH * (odd + 1))
+    def quantize(codes, plane, lo, col):
+        return done("v", v.quantize_mx(codes[:, lo:lo + SH], plane[:, lo:lo + SH], T.md[:, 4 * col:4 * col + 4 * SH]))
+
     wait("v", "lwm", 16)
-    v_qw = done("v", v.quantize_mx(T.c1[:, wq], T.p1[:, wq], T.md[:, 4 * wcol:4 * wcol + 4 * SH]))
+    v_qw = quantize(T.c1, T.p1, columns(slot, r, "w")[0], wcol)
     wait("v", "lix", 128)
     a = done("v", v.tensor_copy(T.o1[:], T.ix[:]))
     v_o4 = done("v", v.tensor_scalar(T.o4[:], T.ix[:, 0:4], 4, None, mult))
@@ -242,8 +257,8 @@ def rank_program(g, core, T, topo):
     def carry(t, after):
         wait("s", "v", after)
         a = done("s", sc.activation(table(t + 1), table(t), Ident, bias=float(CH)))
-        b = done("s", sc.activation(T.lk[:, CH * (t - 1):CH * t], table(t).indirect(T.o1[:, 4 * t:4 * t + 4]), Copy))
-        return a, b
+        done("s", sc.activation(T.lk[:, CH * (t - 1):CH * t], table(t).indirect(T.o1[:, 4 * t:4 * t + 4]), Copy))
+        return a
 
     def first(e):
         return done("v", v.tensor_tensor(T.md[:, 4 * dcol[1] + e:4 * dcol[1] + 4 * CH:4],
@@ -253,31 +268,26 @@ def rank_program(g, core, T, topo):
     s_d1 = scale(1, "ld1")
     wait("v", "v", a)
     wait("v", "g", g_vl)
-    a = place(1)
-    s_t2, _ = carry(1, a)
-    s_d2 = scale(2, "ld2")
+    s_t2 = carry(1, place(1))
     wait("v", "v", v_o4)
     wait("v", "s", s_d1)
     first(0)
     first(1)
     wait("v", "s", s_t2)
-    a = place(2)
-    s_t3, _ = carry(2, a)
+    s_t3 = carry(2, place(2))
     first(2)
     v_d1 = first(3)
     wait("v", "s", s_t3)
-    a = place(3)
-    wait("s", "v", a)
-    s_lk = done("s", sc.activation(T.lk[:, 128:176], T.tb[:].indirect(T.co[:, 0:3]), Copy))
+    wait("s", "v", place(3))
+    s_lk = done("s", sc.activation(T.lk[:, 2 * CH:LK], T.tb[:].indirect(T.co[:, 0:3]), Copy))
+    s_d2 = scale(2, "ld2")
     s_d3 = scale(3, "ld2")
-    q1 = slice(a1 + (S1 - 2 * CH) * odd, a1 + (S1 - 2 * CH) * odd + 2 * CH)
-    m1 = min(dcol[1], dcol[2])
     wait("v", "v", v_d1)
-    v_q1 = done("v", v.quantize_mx(T.c1[:, q1], T.p1[:, q1], T.md[:, 4 * m1:4 * m1 + 8 * CH]))
+    v_q1 = quantize(T.c1, T.p1, S1 * own + (S1 - SH) * odd, min(dcol[1], dcol[2]))
     wait("v", "s", s_lk)
     a = done("v", v.tensor_tensor_scan(T.sn[:], T.cs[:], T.lk[:], 0.0, add, AluOpType.min))
     wait("v", "v", a)
-    v_ls = done("v", v.tensor_scalar(T.ls[:], T.sn[:, 143:176:16], T.lc[:], None, add))
+    v_ls = done("v", v.tensor_scalar(T.ls[:], T.sn[:, 2 * CH + 15:LK:16], T.lc[:], None, add))
     done("v", v.tensor_scalar(T.o2[:], T.sn[:, 3:CH:4], 4, T.e2[:], mult, add))
     done("v", v.tensor_scalar(T.o3[:], T.sn[:, CH + 3:2 * CH:4], 4, T.e3[:], mult, add))
     for k, s in ((2, s_d2), (3, s_d3)):
@@ -286,42 +296,38 @@ def rank_program(g, core, T, topo):
         wait("v", "s", s)
         done("v", v.tensor_tensor(T.md[:, 4 * dcol[k]:4 * dcol[k] + 4 * CH], T.md[:, 4 * lo:4 * hi].indirect(T["o%d" % k][:]),
                                   T.dls[:, 4 * CH * (k - 1):4 * CH * k], add))
-    q2 = slice(a2 + 2 * CH * odd, a2 + 2 * CH * (odd + 1))
-    m2 = min(dcol[2], dcol[3])
     wait("v", "v", cnt["v"])
-    v_q2 = done("v", v.quantize_mx(T.c2[:, q2], T.p2[:, q2], T.md[:, 4 * m2:4 * m2 + 8 * CH]))
+    v_q2 = quantize(T.c2, T.p2, columns(slot, r, "e")[0], min(dcol[2], dcol[3]))
     wait("v", "lx", 16)
-    v_qx = done("v", v.quantize_mx(T.xq[:], T.xs[:], T.xt[:]))
+    v_qx = [done("v", v.quantize_mx(T.xq[:], T.xs[:], T.xt[:]))] * 4
 
-    others = [T.cores[q] for q in range(N) if q != r]
+    others = [T.cores[(r + k) % N] for k in range(1, N)]
     out = topo.engines(core, others[0])
     nloc = [0]
 
-    def send(piece):
-        view = piece_view(T, slot, r, piece)
-        dst = [T.cores[q] for q in direct[r]] + [carrier(stage, piece) for stage in stages[r]]
-        off = [c for c in dst if topo.chip(c) != topo.chip(core)]
-        on = [c for c in dst if topo.chip(c) == topo.chip(core)]
-        rest = [e for e in topo.engines(core, on[0]) if e not in out]
-        g.remote_dma_fused([RemoteDMATransfer(dst_ids=[dst_id(c, topo) for c in d], dma_engine_mask=bits(e),
-                                              remote_sem=T.sem["a%s%d" % (piece, r)], srcs=[view], dsts=[view for _ in d])
-                            for d, e in ((on, rest), (off, out))], local_sem=T.sem.loc)
-        nloc[0] += len(rest) + len(out)
+    def send(phase, after):
+        wait("g", "v", after)
+        for piece in PHASE[phase]:
+            view = piece_view(T, slot, r, piece)
+            dst = [carrier(stage, piece) for stage in stages[r]] + [T.cores[q] for q in direct[r]]
+            off = [c for c in dst if topo.chip(c) != topo.chip(core)]
+            on = [c for c in dst if topo.chip(c) == topo.chip(core)]
+            rest = [e for e in topo.engines(core, on[0]) if e not in out]
+            tr = [RemoteDMATransfer(dst_ids=[dst_id(c, topo) for c in d], dma_engine_mask=bits(e),
+                                    remote_sem=T.sem["a%s%d" % (piece, r)], srcs=[view],
+                                    dsts=[view for _ in d]) for d, e in ((on, rest), (off, out))]
+            g.remote_dma_fused(tr, local_sem=T.sem.loc)
+            nloc[0] += len(rest) + len(out)
 
     land = T.lland[128 * r:128 * (r + 1), :]
-    wait("g", "v", v_qw)
-    send("A")
-    wait("g", "v", v_q1)
-    send("B")
-    send("C")
+    send("w", v_qw)
+    send("u", v_q1)
     wait("g", "v", v_ls)
     g.remote_dma_fused([RemoteDMATransfer(dst_ids=[dst_id(c, topo) for c in others], dma_engine_mask=bits(out),
-                                          remote_sem=T.sem.lst, srcs=[T.ls[:]], dsts=[land for _ in others])],
+                                          remote_sem=T.sem["l%d" % r], srcs=[T.ls[:]], dsts=[land for _ in others])],
                        local_sem=T.sem.loc)
     nloc[0] += len(out)
-    wait("g", "v", v_q2)
-    send("D")
-    send("E")
+    send("e", v_q2)
 
     def lay(q):
         c = 16 * slot[q][0] + 8 * slot[q][1]
@@ -332,101 +338,107 @@ def rank_program(g, core, T, topo):
     y.dma_start(land, T.ls[:]).then_inc(T.sem.lbo, 16)
     wait("y", "lbo", 16)
     lay(r)
-    wait("y", "lst", len(out) * (N - 1))
-    for q in range(N):
-        if q != r:
-            lay(q)
+    for k in range(1, N):
+        wait("y", "l%d" % ((r - k) % N), len(out))
+        lay((r - k) % N)
 
-    A, B, C = own, (own - 1) % NP, (own + 1) % NP
-    order = (B, A, C)
-    units = [(1, p, t) for p in order for t in (1, 0, 3, 2)] + [(2, p, t) for p in order for t in (3, 2)]
-    eng = {u: "v" if u[2] % 2 else "s" for u in units}
-    bank, use = {}, {"v": 0, "s": 0}
-    for u in units:
-        e = eng[u]
-        bank[u] = (0 if e == "v" else 4) + use[e] % 4
-        use[e] += 1
-    num = {u: i + 1 for i, u in enumerate(units)}
-
-    def ps(u, lo, hi):
-        return T.pb[:, 512 * bank[u] + lo:512 * bank[u] + hi]
+    use, last, drained, stores = {"v": 0, "s": 0}, {}, {}, [0]
+    ready = {}
 
     def copy(e, out, in_):
         return done(e, v.tensor_copy(out, in_) if e == "v" else sc.activation(out, in_, Copy))
 
-    drained, got, spread = {}, {}, [0]
+    load = {"v": 0, "s": 0}
 
-    def drain(*u):
-        ph, p, t = u
-        e = eng[u]
-        wait(e, "p", num[u])
-        if t == 0:
-            drained[u] = copy(e, T.y0[:, 256 * p:256 * p + 256], ps(u, 0, 256))
-            got[(p, 0)] = (e, drained[u])
-            return
-        pw, lo, n = T["pw%d" % t], win(t) * p, CH * (t - 1)
-        if ph == 1:
-            drained[u] = copy(e, pw[:, lo + n:lo + n + win(1)], ps(u, 0, win(1)))
+    def engine(elements):
+        e = "v" if load["v"] <= load["s"] else "s"
+        load[e] += elements
+        return e
+
+    def product(phase, qs, t):
+        p, s = slot[qs[0]]
+        lo, n = columns(slot, qs[0], phase)
+        n *= len(qs)
+        e = engine(CH * (t - 1) * len(qs) if phase == "e" else n)
+        bank = (0 if e == "v" else 4) + use[e] % 4
+        use[e] += 1
+        wait("p", "v", v_q2 if phase == "e" else v_qx[t])
+        for q in qs:
+            if q != r:
+                for piece in PHASE[phase] + (PHASE["w"] if phase == "u" else ""):
+                    wait("p", "a%s%d" % (piece, q), 8)
+        if bank in last:
+            wait("p", e, last[bank])
+        mid, m = win(t) * p + win(t) // 2, CH * (t - 1)
+        if phase != "e":
+            runs = [(0, n, mid if s else mid - n // len(qs))]
+        elif len(qs) == 2:
+            lo, n = lo + 2 * CH - m, 2 * m
+            runs = [(0, m, win(t) * p), (m, m, win(t) * (p + 1) - m)]
         else:
-            copy(e, pw[:, lo:lo + n], ps(u, 0, n))
-            drained[u] = copy(e, pw[:, lo + win(t) - n:lo + win(t)], ps(u, n, 2 * n))
+            runs = [(0, m, win(t) * (p + 1) - m)] if s else [(2 * CH - m, m, win(t) * p)]
+        codes, plane = (T.c2, T.p2) if phase == "e" else (T.c1, T.p1)
+        k = done("p", te.matmul_mx(T.pb[:, 512 * bank:512 * bank + n], T.xq[:, 128 * t:128 * t + 128],
+                                   T.xs[:, 128 * t:128 * t + 128], codes[:, lo:lo + n], plane[:, lo:lo + n], True, True))
+        wait(e, "p", k)
+        for a, w, to in runs:
+            last[bank] = copy(e, T["pw%d" % t if t else "y0"][:, to:to + w], T.pb[:, 512 * bank + a:512 * bank + a + w])
+        ready.setdefault((p, t), {})[e] = last[bank]
 
-    def gather(e, p, t):
-        wait(e, "v", spread[0])
-        u = (1 if t == 1 else 2, p, t)
-        wait(e, eng[u], drained[u])
+    def products(phase, ranks):
+        groups = []
+        for q in ranks:
+            if all(x in ranks for x in pairs[slot[q][0]]):
+                if slot[q][1] == 0:
+                    groups.append(pairs[slot[q][0]])
+            else:
+                groups.append((q,))
+        for qs in groups:
+            for t in {"w": (0,), "u": (1, 2, 3), "e": (3, 2)}[phase]:
+                product(phase, qs, t)
+
+    def store(p, t, after, on="y"):
+        for e, k in after.items():
+            wait(on, e, k)
+        a, b = pairs[p]
+        for q, lo, n in ([(a, 0, 2 * SH)] if b == a + 1 else [(a, 0, SH), (b, SH, SH)]):
+            queue[on].dma_start(T.y[:, SH * (N * t + q):SH * (N * t + q) + n],
+                                T["y%d" % t][:, 256 * p + lo:256 * p + lo + n]).then_inc(T.sem.stz, 16)
+            stores[0] += 1
+
+    def gather(p, t, last=False):
+        e = engine(7 * CH)
+        wait(e, "v", spread)
+        for f, k in ready[(p, t)].items():
+            wait(e, f, k)
         window = T["pw%d" % t][:, win(t) * p:win(t) * (p + 1)].indirect(T.offs[:, t - 1, 16 * p:16 * p + 16])
-        got[(p, t)] = (e, copy(e, T["y%d" % t][:, 256 * p:256 * p + 256], window))
+        store(p, t, {e: copy(e, T["y%d" % t][:, 256 * p:256 * p + 256], window)}, "s" if last and e == "s" else "y")
 
-    for p in (B, A):
-        for t in (1, 0, 3, 2):
-            drain(1, p, t)
+    order = [(own - 1) % NP, own, (own + 1) % NP]
+    early = [q for q in range(N) if r in direct[q]]
+    late = [q for p in order for q in pairs[p] if q != r and q not in early]
+    for ranks in ([r], early):
+        products("w", ranks)
+        products("u", ranks)
+    products("e", [r])
+    products("w", late)
+    for p in order:
+        store(p, 0, ready[(p, 0)])
+    load["v"] = load["s"] = 0
+    products("u", late)
+    products("e", early)
     wait("v", "st2", 32 * N)
     for k in (1, 2, 3):
-        spread[0] = done("v", v.tensor_copy(T.offs[32 * k:32 * k + 32, :, :], T.offs[0:32, :, :]))
-    gather("v", B, 1)
-    for t in (1, 0, 3, 2):
-        drain(1, C, t)
-    gather("s", A, 1)
-    gather("s", C, 1)
+        spread = copy("v", T.offs[32 * k:32 * k + 32, :, :], T.offs[0:32, :, :])
+    load["v"] += 3 * CH
     for p in order:
-        for t in (3, 2):
-            drain(2, p, t)
-            gather(eng[(2, p, t)], p, t)
-
-    wait("p", "v", v_qx)
-    last = {}
-    for u in units:
-        ph, p, t = u
-        for q in pairs[p]:
-            if q != r:
-                for piece in ("ABC" if ph == 1 else "DE"):
-                    wait("p", "a%s%d" % (piece, q), 8)
-        b = bank[u]
-        if b in last:
-            wait("p", eng[u], drained[last[b]])
-        last[b] = u
-        if ph == 1:
-            n = 2 * SH if t == 0 else win(1)
-            lo, codes, scales = S1 * p + (S1 - n) // 2, T.c1, T.p1
-        else:
-            n = 2 * CH * (t - 1)
-            lo, codes, scales = S2 * p + (S2 - n) // 2, T.c2, T.p2
-        done("p", te.matmul_mx(ps(u, 0, n), T.xq[:, 128 * t:128 * t + 128], T.xs[:, 128 * t:128 * t + 128],
-                               codes[:, lo:lo + n], scales[:, lo:lo + n], True, True))
-
-    stores = 0
-    for p, t in [(B, 0), (A, 0), (B, 1), (C, 0), (A, 1), (C, 1)] + [(p, t) for p in order for t in (2, 3)]:
-        e, k = got[(p, t)]
-        wait("y", e, k)
-        a, b = pairs[p]
-        runs = [(a, 0, 2 * SH)] if b == a + 1 else [(a, 0, SH), (b, SH, SH)]
-        for q, lo, n in runs:
-            y.dma_start(T.y[:, SH * (N * t + q):SH * (N * t + q) + n],
-                        T["y%d" % t][:, 256 * p + lo:256 * p + lo + n]).then_inc(T.sem.stz, 16)
-            stores += 1
+        gather(p, 1)
+    for p in order:
+        products("e", [q for q in late if slot[q][0] == p])
+        gather(p, 3, p == order[-1])
+        gather(p, 2, p == order[-1])
 
     wait("g", "loc", nloc[0])
     for k in ("g", "v", "s", "p"):
         wait("g", k, cnt[k])
-    wait("g", "stz", 16 * stores)
+    wait("g", "stz", 16 * stores[0])

import numpy as np
from concourse.bass import DstId, RemoteDMATransfer
from concourse.mybir import dt, AluOpType, ActivationFunctionType

N, SH, CH, RD = 6, 128, 64, 4
NP = N // 2
S1, S2 = 2 * SH + 4 * CH, 4 * CH
BIG = 1024.0
LK = 2 * CH + 48
F8 = "float8_e4m3fn_x4"
PIECES = "ABCDEF"
PHASE = {"w": "AB", "u": "CD", "e": "EF"}


def win(t):
    return 2 * SH + 2 * CH * t


SCRATCH = {
    "md": ("sbuf", [128, 4 * (SH + 3 * CH)], "bfloat16"),
    "dlt": ("sbuf", [128, 3 * 4 * CH], "bfloat16"),
    "dls": ("sbuf", [128, 3 * 4 * CH], "bfloat16"),
    "xt": ("sbuf", [128, RD * 512], "bfloat16"),
    "xq": ("sbuf", [128, RD * 128], F8),
    "xs": ("sbuf", [128, RD * 128], "uint8"),
    "c1": ("sbuf", [128, NP * S1], F8),
    "p1": ("sbuf", [128, NP * S1], "uint8"),
    "c2": ("sbuf", [128, NP * S2], F8),
    "p2": ("sbuf", [128, NP * S2], "uint8"),
    "ix": ("sbuf", [128, 12], "int32"),
    "o1": ("sbuf", [128, 12], "uint16"),
    "o4": ("sbuf", [128, 4], "uint16"),
    "o2": ("sbuf", [128, 16], "uint16"),
    "o3": ("sbuf", [128, 16], "uint16"),
    "pi": ("sbuf", [128, 1], "int32"),
    "pa": ("sbuf", [128, 1], "int32"),
    "pe": ("sbuf", [128, 1], "int32"),
    "pf": ("sbuf", [128, 1], "float32"),
    "lc": ("sbuf", [128, 1], "float32"),
    "ec": ("sbuf", [128, 1], "float32"),
    "e2": ("sbuf", [128, 1], "float32"),
    "e3": ("sbuf", [128, 1], "float32"),
    "jj": ("sbuf", [128, 4], "int32"),
    "co": ("sbuf", [128, 4], "uint16"),
    "mi": ("sbuf", [128, 32], "int32"),
    "mj": ("sbuf", [128, 32], "int32"),
    "ma": ("sbuf", [128, 32], "float32"),
    "mb": ("sbuf", [128, 32], "float32"),
    "cs": ("sbuf", [128, LK], "float32"),
    "vl": ("sbuf", [128, 3 * CH], "float32"),
    "tb": ("sbuf", [128, 3 * SH], "float32"),
    "lk": ("sbuf", [128, LK], "float32"),
    "sn": ("sbuf", [128, LK], "float32"),
    "ls": ("sbuf", [128, 3], "uint16"),
    "lland": ("dram", [N * 128, 3], "uint16"),
    "offs": ("sbuf", [128, 3, 8 * N], "uint16"),
    "pw1": ("sbuf", [128, NP * win(1)], "float32"),
    "pw2": ("sbuf", [128, NP * win(2)], "float32"),
    "pw3": ("sbuf", [128, NP * win(3)], "float32"),
    "y0": ("sbuf", [128, N * SH], "float32"),
    "y1": ("sbuf", [128, N * SH], "float32"),
    "y2": ("sbuf", [128, N * SH], "float32"),
    "y3": ("sbuf", [128, N * SH], "float32"),
    "pb": ("psum", [128, 512 * 8], "float32"),
}
SEMAPHORES = (["vs", "ss", "ps", "gs", "lix", "lwm", "ld1", "ld2", "lx", "lbo", "st2", "stz", "loc"] + ["l%d" % q for q in range(N)]
              + ["a%s%d" % (p, q) for p in PIECES for q in range(N)])


def bits(engines):
    m = 0
    for e in engines:
        m |= 1 << e
    return m


def routes(cores, topo):
    chips = [topo.chip(c) for c in cores]
    pairs = [(a, b) for a in range(N) for b in range(a + 1, N) if topo.mates(chips[a], chips[b])]
    rest = [a for a in range(N) if all(a not in p for p in pairs)]
    pairs += [(rest[i], rest[i + 1]) for i in range(0, len(rest), 2)]
    slot = {q: (k, s) for k in range(NP) for s, q in enumerate(pairs[k])}
    direct = {q: list(pairs[(slot[q][0] + 1) % NP]) for q in range(N)}
    far = {q: [r for r in range(N) if r != q and r not in direct[q]] for q in range(N)}
    near = {q: [] for q in range(N)}
    stages = {q: [] for q in range(N)}
    for r in rest:
        k, s = slot[r]
        mate = [c for c in range(topo.CHIPS * topo.CORES_PER_CHIP) if topo.mates(topo.chip(c), chips[r])]
        q = [q for q in range(N) if r in direct[q] and topo.same_plane(chips[q], topo.chip(mate[0]))][0]
        direct[q].remove(r)
        ok = [c for c in mate if topo.may_write(c, cores[r])]
        stages[q].append(([ok[0], ok[-1]], [r]))
    for a, b in pairs:
        for q, r in ((a, b), (b, a)):
            far[q].remove(r)
            near[q].append(r)
    for q in range(N):
        for dsts, same in ((far[q], False), (near[q], True)):
            if dsts:
                ok = [c for c in topo.cores_of(cores[q]) if c != cores[q] and (topo.die(c) == topo.die(cores[q])) == same
                      and all(topo.may_write(c, cores[r]) for r in dsts)]
                stages[q].append((ok[:2], dsts))
    return pairs, slot, direct, stages


_CACHE = {}


def plan(T, topo):
    if "r" not in _CACHE:
        _CACHE["r"] = routes(list(T.cores), topo)
    return _CACHE["r"]


def carrier(stage, piece):
    return stage[0][0] if piece in "ACF" else stage[0][-1]


def dst_id(c, topo):
    rid, pid, _ = topo.addr(c)
    return DstId(rid=rid, pnc=pid)


def columns(slot, q, phase):
    k, s = slot[q]
    if phase == "w":
        return S1 * k + 2 * CH + SH * s, SH
    if phase == "d":
        return S1 * k + (2 * CH + 2 * SH if s else CH), CH
    if phase == "u":
        return S1 * k + CH + (SH + CH) * s, SH + CH
    return S2 * k + 2 * CH * s, 2 * CH


def piece_view(T, slot, q, piece):
    lo, n = columns(slot, q, "wwddee"[PIECES.index(piece)])
    if piece in "ACE":
        return (T.c2 if piece == "E" else T.c1)[:, lo:lo + n].bitcast(dt.uint8)
    return (T.p2 if piece == "F" else T.p1)[:, lo:lo + n]


def helper_program(g, core, T, topo, slot, q, stage):
    dst = [T.cores[r] for r in stage[1]]
    eng = [e for e in topo.engines(core, dst[0]) if all(e in topo.engines(core, d) for d in dst)]
    n = 0
    for piece in PIECES:
        if carrier(stage, piece) == core:
            s, view = T.sem["a%s%d" % (piece, q)], piece_view(T, slot, q, piece)
            g.wait_ge(s, 8)
            g.remote_dma_fused([RemoteDMATransfer(dst_ids=[dst_id(c, topo) for c in dst], dma_engine_mask=bits(eng),
                                                  remote_sem=s, srcs=[view], dsts=[view for _ in dst])],
                               local_sem=T.sem.loc)
            n += len(eng)
    g.wait_ge(T.sem.loc, n)


def rank_program(g, core, T, topo):
    pairs, slot, direct, stages = plan(T, topo)
    r = T.rank_of(core)
    if r is None:
        for q in range(N):
            for stage in stages[q]:
                if core in stage[0]:
                    helper_program(g, core, T, topo, slot, q, stage)
        return
    own, odd = slot[r]
    wcol = 0 if odd else 3 * CH
    dcol = [None] + [(SH + CH * (k - 1)) if odd else CH * (3 - k) for k in (1, 2, 3)]
    add, mult = AluOpType.add, AluOpType.mult
    band, shr = AluOpType.bitwise_and, AluOpType.arith_shift_right
    cnt = {"v": 0, "s": 0, "p": 0, "g": 0}
    sem = {"v": T.sem.vs, "s": T.sem.ss, "p": T.sem.ps, "g": T.sem.gs}
    queue = {"v": g.vector, "s": g.scalar, "p": g.tensor, "g": g, "y": g.sync}
    seen = {}

    def done(k, ins):
        ins.then_inc(sem[k], 1)
        cnt[k] += 1
        return cnt[k]

    def wait(on, s, val):
        key = (on, s)
        if seen.get(key, 0) < val:
            seen[key] = val
            queue[on].wait_ge(sem[s] if s in sem else T.sem[s], val)

    v, sc, y, te = g.vector, g.scalar, g.sync, g.tensor
    Copy, Ident = ActivationFunctionType.Copy, ActivationFunctionType.Identity

    y.dma_start(T.md[:, 4 * wcol:4 * wcol + 4 * SH], T.wm[:]).then_inc(T.sem.lwm, 16)
    for k in range(4):
        y.dma_start(T.ix[16 * k:16 * k + 16, :], T.idx[:]).then_inc(T.sem.lix, 16)
        sc.dma_start(T.ix[64 + 16 * k:64 + 16 * k + 16, :], T.idx[:]).then_inc(T.sem.lix, 16)
    y.dma_start(T.dlt[:, 0:4 * CH], T.dl[:, 0:4 * CH]).then_inc(T.sem.ld1, 16)
    sc.dma_start(T.dlt[:, 4 * CH:12 * CH], T.dl[:, 4 * CH:12 * CH]).then_inc(T.sem.ld2, 16)
    sc.dma_start(T.xt[:], T.x[:]).then_inc(T.sem.lx, 16)

    small = {"allow_small_or_imprecise_dtypes": True}
    g_pi = done("g", g.iota(T.pi[:], [[0, 1]], 0, 1))
    done("g", g.iota(T.mi[:, 16:32], [[1, 16]], 128, -1))
    g_mi = done("g", g.iota(T.mi[:, 0:16], [[4, 16]], 512 + 3, -1))
    g_jj = done("g", g.iota(T.jj[:, 0:3], [[16, 3]], 0, 48))
    g_v1 = done("g", g.iota(T.vl[:, 0:CH], [[1, CH]], (CH + 2 * SH) * odd, 0, **small))
    g_vl = done("g", g.iota(T.tb[:, 0:SH], [[1, SH]], CH + SH * odd, 0, **small))

    done("v", v.memset(T.md[:, 4 * dcol[2]:4 * dcol[2] + 4 * CH], 0.0))
    wait("v", "g", g_pi)
    done("v", v.tensor_scalar(T.pa[:], T.pi[:], 3, None, shr))
    a = done("v", v.tensor_scalar(T.pe[:], T.pi[:], 3, None, band))
    wait("v", "v", a)
    done("v", v.tensor_scalar(T.pf[:], T.pa[:], 1 - 3 * SH, None, mult))
    wait("v", "g", g_mi)
    done("v", v.tensor_scalar(T.mj[:, 16:32], T.mi[:, 16:32], 15, None, band))
    a = done("v", v.tensor_scalar(T.mj[:, 0:16], T.mi[:, 0:16], 2, 3, shr, band))
    wait("v", "v", a)
    done("v", v.tensor_scalar(T.ma[:], T.mj[:], 0, 3 * BIG, AluOpType.is_equal, mult))
    a = done("v", v.tensor_scalar(T.mb[:], T.mj[:], 1, -BIG, AluOpType.is_equal, mult))
    wait("v", "g", g_jj)
    done("v", v.tensor_scalar(T.co[:, 0:3], T.jj[:, 0:3], T.pf[:], None, add))
    wait("v", "v", a)
    done("v", v.tensor_tensor(T.cs[:, 0:16], T.ma[:, 0:16], T.mb[:, 0:16], add))
    v_cs = done("v", v.tensor_tensor(T.cs[:, 2 * CH:2 * CH + 16], T.ma[:, 16:32], T.mb[:, 16:32], add))
    done("v", v.tensor_scalar(T.lc[:], T.ma[:, 31:32], 1, BIG, AluOpType.is_lt, mult))
    a = done("v", v.tensor_scalar(T.ec[:], T.ma[:, 3:4], 1, 4 * BIG, AluOpType.is_lt, mult))
    wait("s", "g", g_v1)
    for t in (1, 2):
        done("s", sc.activation(T.vl[:, CH * t:CH * (t + 1)], T.vl[:, 0:CH], Ident, bias=float(2 * CH * t * odd)))
    wait("s", "v", v_cs)
    for lo, n, to in ((0, 16, 16), (2 * CH, 16, 2 * CH + 16), (2 * CH, 16, 2 * CH + 32), (0, 32, 32), (0, 64, 64)):
        wait("s", "s", cnt["s"] - (2 if n == 32 else 0 if n == 64 else cnt["s"]))
        done("s", sc.activation(T.cs[:, to:to + n], T.cs[:, lo:lo + n], Copy))
    wait("v", "v", a)
    done("v", v.tensor_scalar(T.e2[:], T.pe[:], T.ec[:], -4 * 3 * CH * odd, add, add))
    done("v", v.tensor_scalar(T.e3[:], T.pe[:], T.ec[:], -4 * 4 * CH * odd, add, add))

    def quantize(codes, plane, lo, col):
        return done("v", v.quantize_mx(codes[:, lo:lo + SH], plane[:, lo:lo + SH], T.md[:, 4 * col:4 * col + 4 * SH]))

    wait("v", "lwm", 16)
    v_qw = quantize(T.c1, T.p1, columns(slot, r, "w")[0], wcol)
    wait("v", "lix", 128)
    a = done("v", v.tensor_copy(T.o1[:], T.ix[:]))
    v_o4 = done("v", v.tensor_scalar(T.o4[:], T.ix[:, 0:4], 4, None, mult))

    def scale(k, s):
        wait("s", s, 16)
        sl = slice(4 * CH * (k - 1), 4 * CH * k)
        return done("s", sc.activation(T.dls[:, sl], T.dlt[:, sl], Copy, scale=0.25))

    def table(t):
        return T.tb[:, SH * (t - 1):SH * t]

    def place(t):
        return done("v", v.tensor_copy(table(t).indirect(T.o1[:, 4 * (t - 1):4 * t]), T.vl[:, CH * (t - 1):CH * t]))

    def carry(t, after):
        wait("s", "v", after)
        a = done("s", sc.activation(table(t + 1), table(t), Ident, bias=float(CH)))
        done("s", sc.activation(T.lk[:, CH * (t - 1):CH * t], table(t).indirect(T.o1[:, 4 * t:4 * t + 4]), Copy))
        return a

    def first(e):
        return done("v", v.tensor_tensor(T.md[:, 4 * dcol[1] + e:4 * dcol[1] + 4 * CH:4],
                                         T.md[:, 4 * wcol + e:4 * wcol + 4 * SH].indirect(T.o4[:]),
                                         T.dls[:, e:4 * CH:4], add))

    s_d1 = scale(1, "ld1")
    wait("v", "v", a)
    wait("v", "g", g_vl)
    s_t2 = carry(1, place(1))
    wait("v", "v", v_o4)
    wait("v", "s", s_d1)
    first(0)
    first(1)
    wait("v", "s", s_t2)
    s_t3 = carry(2, place(2))
    first(2)
    v_d1 = first(3)
    wait("v", "s", s_t3)
    wait("s", "v", place(3))
    s_lk = done("s", sc.activation(T.lk[:, 2 * CH:LK], T.tb[:].indirect(T.co[:, 0:3]), Copy))
    s_d2 = scale(2, "ld2")
    s_d3 = scale(3, "ld2")
    wait("v", "v", v_d1)
    v_q1 = quantize(T.c1, T.p1, S1 * own + (S1 - SH) * odd, min(dcol[1], dcol[2]))
    wait("v", "s", s_lk)
    a = done("v", v.tensor_tensor_scan(T.sn[:], T.cs[:], T.lk[:], 0.0, add, AluOpType.min))
    wait("v", "v", a)
    v_ls = done("v", v.tensor_scalar(T.ls[:], T.sn[:, 2 * CH + 15:LK:16], T.lc[:], None, add))
    done("v", v.tensor_scalar(T.o2[:], T.sn[:, 3:CH:4], 4, T.e2[:], mult, add))
    done("v", v.tensor_scalar(T.o3[:], T.sn[:, CH + 3:2 * CH:4], 4, T.e3[:], mult, add))
    for k, s in ((2, s_d2), (3, s_d3)):
        lo, hi = (0, dcol[k]) if odd else (dcol[k] + CH, SH + 3 * CH)
        wait("v", "v", cnt["v"] - (3 - k))
        wait("v", "s", s)
        done("v", v.tensor_tensor(T.md[:, 4 * dcol[k]:4 * dcol[k] + 4 * CH], T.md[:, 4 * lo:4 * hi].indirect(T["o%d" % k][:]),
                                  T.dls[:, 4 * CH * (k - 1):4 * CH * k], add))
    wait("v", "v", cnt["v"])
    v_q2 = quantize(T.c2, T.p2, columns(slot, r, "e")[0], min(dcol[2], dcol[3]))
    wait("v", "lx", 16)
    v_qx = [done("v", v.quantize_mx(T.xq[:], T.xs[:], T.xt[:]))] * 4

    others = [T.cores[(r + k) % N] for k in range(1, N)]
    out = topo.engines(core, others[0])
    nloc = [0]

    def send(phase, after):
        wait("g", "v", after)
        for piece in PHASE[phase]:
            view = piece_view(T, slot, r, piece)
            dst = [carrier(stage, piece) for stage in stages[r]] + [T.cores[q] for q in direct[r]]
            off = [c for c in dst if topo.chip(c) != topo.chip(core)]
            on = [c for c in dst if topo.chip(c) == topo.chip(core)]
            rest = [e for e in topo.engines(core, on[0]) if e not in out]
            tr = [RemoteDMATransfer(dst_ids=[dst_id(c, topo) for c in d], dma_engine_mask=bits(e),
                                    remote_sem=T.sem["a%s%d" % (piece, r)], srcs=[view],
                                    dsts=[view for _ in d]) for d, e in ((on, rest), (off, out))]
            g.remote_dma_fused(tr, local_sem=T.sem.loc)
            nloc[0] += len(rest) + len(out)

    land = T.lland[128 * r:128 * (r + 1), :]
    send("w", v_qw)
    send("u", v_q1)
    wait("g", "v", v_ls)
    g.remote_dma_fused([RemoteDMATransfer(dst_ids=[dst_id(c, topo) for c in others], dma_engine_mask=bits(out),
                                          remote_sem=T.sem["l%d" % r], srcs=[T.ls[:]], dsts=[land for _ in others])],
                       local_sem=T.sem.loc)
    nloc[0] += len(out)
    send("e", v_q2)

    def lay(q):
        c = 16 * slot[q][0] + 8 * slot[q][1]
        for h in range(2):
            y.dma_start(T.offs[16 * h:16 * h + 16, :, c:c + 8], T.lland[128 * q:128 * (q + 1), :]).then_inc(T.sem.st2, 16)

    wait("y", "v", v_ls)
    y.dma_start(land, T.ls[:]).then_inc(T.sem.lbo, 16)
    wait("y", "lbo", 16)
    lay(r)
    for k in range(1, N):
        wait("y", "l%d" % ((r - k) % N), len(out))
        lay((r - k) % N)

    use, last, drained, stores = {"v": 0, "s": 0}, {}, {}, [0]
    ready = {}

    def copy(e, out, in_):
        return done(e, v.tensor_copy(out, in_) if e == "v" else sc.activation(out, in_, Copy))

    load = {"v": 0, "s": 0}

    def engine(elements):
        e = "v" if load["v"] <= load["s"] else "s"
        load[e] += elements
        return e

    def product(phase, qs, t):
        p, s = slot[qs[0]]
        lo, n = columns(slot, qs[0], phase)
        n *= len(qs)
        e = engine(CH * (t - 1) * len(qs) if phase == "e" else n)
        bank = (0 if e == "v" else 4) + use[e] % 4
        use[e] += 1
        wait("p", "v", v_q2 if phase == "e" else v_qx[t])
        for q in qs:
            if q != r:
                for piece in PHASE[phase] + (PHASE["w"] if phase == "u" else ""):
                    wait("p", "a%s%d" % (piece, q), 8)
        if bank in last:
            wait("p", e, last[bank])
        mid, m = win(t) * p + win(t) // 2, CH * (t - 1)
        if phase != "e":
            runs = [(0, n, mid if s else mid - n // len(qs))]
        elif len(qs) == 2:
            lo, n = lo + 2 * CH - m, 2 * m
            runs = [(0, m, win(t) * p), (m, m, win(t) * (p + 1) - m)]
        else:
            runs = [(0, m, win(t) * (p + 1) - m)] if s else [(2 * CH - m, m, win(t) * p)]
        codes, plane = (T.c2, T.p2) if phase == "e" else (T.c1, T.p1)
        k = done("p", te.matmul_mx(T.pb[:, 512 * bank:512 * bank + n], T.xq[:, 128 * t:128 * t + 128],
                                   T.xs[:, 128 * t:128 * t + 128], codes[:, lo:lo + n], plane[:, lo:lo + n], True, True))
        wait(e, "p", k)
        for a, w, to in runs:
            last[bank] = copy(e, T["pw%d" % t if t else "y0"][:, to:to + w], T.pb[:, 512 * bank + a:512 * bank + a + w])
        ready.setdefault((p, t), {})[e] = last[bank]

    def products(phase, ranks):
        groups = []
        for q in ranks:
            if all(x in ranks for x in pairs[slot[q][0]]):
                if slot[q][1] == 0:
                    groups.append(pairs[slot[q][0]])
            else:
                groups.append((q,))
        for qs in groups:
            for t in {"w": (0,), "u": (1, 2, 3), "e": (3, 2)}[phase]:
                product(phase, qs, t)

    def store(p, t, after, on="y"):
        for e, k in after.items():
            wait(on, e, k)
        a, b = pairs[p]
        for q, lo, n in ([(a, 0, 2 * SH)] if b == a + 1 else [(a, 0, SH), (b, SH, SH)]):
            queue[on].dma_start(T.y[:, SH * (N * t + q):SH * (N * t + q) + n],
                                T["y%d" % t][:, 256 * p + lo:256 * p + lo + n]).then_inc(T.sem.stz, 16)
            stores[0] += 1

    def gather(p, t, last=False):
        e = engine(7 * CH)
        wait(e, "v", spread)
        for f, k in ready[(p, t)].items():
            wait(e, f, k)
        window = T["pw%d" % t][:, win(t) * p:win(t) * (p + 1)].indirect(T.offs[:, t - 1, 16 * p:16 * p + 16])
        store(p, t, {e: copy(e, T["y%d" % t][:, 256 * p:256 * p + 256], window)}, "s" if last and e == "s" else "y")

    order = [(own - 1) % NP, own, (own + 1) % NP]
    early = [q for q in range(N) if r in direct[q]]
    late = [q for p in order for q in pairs[p] if q != r and q not in early]
    for ranks in ([r], early):
        products("w", ranks)
        products("u", ranks)
    products("e", [r])
    products("w", late)
    for p in order:
        store(p, 0, ready[(p, 0)])
    load["v"] = load["s"] = 0
    products("u", late)
    products("e", early)
    wait("v", "st2", 32 * N)
    for k in (1, 2, 3):
        spread = copy("v", T.offs[32 * k:32 * k + 32, :, :], T.offs[0:32, :, :])
    load["v"] += 3 * CH
    for p in order:
        gather(p, 1)
    for p in order:
        products("e", [q for q in late if slot[q][0] == p])
        gather(p, 3, p == order[-1])
        gather(p, 2, p == order[-1])

    wait("g", "loc", nloc[0])
    for k in ("g", "v", "s", "p"):
        wait("g", k, cnt[k])
    wait("g", "stz", 16 * stores[0])
